import numpy as np, ml_dtypes
CORES = [2,6,10,14,18,22,26,30]
N = 8
BF = ml_dtypes.bfloat16
W, Q, TV, HOP, M = 4096, 192, 6, 3, 8
def parts(rng):
    hi = rng.choice(np.array([64, 128, 192, 256]), (N, 8, 1, W)); p = np.floor(hi * rng.random((N, 8, 16, W)))
    lo = rng.choice(np.array([0, 32, 64, 128, 192]), (N, 8, 1, Q)); y = lo + np.floor((256 - lo) * rng.random((N, 8, 16, Q)))
    L = rng.integers(0, W, (N, 8, 16, Q)); share = rng.choice(np.array([0.0, 0.1, 0.3, 0.7, 1.0]), (N, 8, 1, Q))
    C = np.where(rng.random((N, 8, 16, Q)) < share, rng.integers(0, W, (N, 8, 16, Q)), -1)
    o = rng.integers(0, 16, (N, 8, 16, Q)); b = np.minimum(rng.integers(0, 8, (N, 8, 16, Q)), rng.integers(0, 8, (N, 8, 16, Q)))
    return p, y, L, C, o, b, rng.integers(0, 4, (N, 8, 16, TV))
def pack(p, y, L, C, o, b, lim):
    def half(a): return np.ascontiguousarray(np.asarray(a, np.float32).reshape(N, 128, -1)).astype(BF)
    def whole(a): return np.ascontiguousarray(np.asarray(a).reshape(N, 128, -1)).astype(np.int32)
    return {"prop": half(p), "lem": whole(L), "con": whole(C), "org": half(o), "cnt": half(b), "ex": half(y), "lim": whole(lim)}
def setup_inputs(rng):
    return pack(*parts(rng))
def setup_inputs_spread(rng):
    p, y, L, C, o, b, lim = parts(rng)
    p = np.minimum(np.floor(np.exp2(8 * rng.random((N, 8, 1, W))) * rng.random((N, 8, 16, W))), 255)
    y = np.minimum(np.floor(np.exp2(2 + 6 * rng.random((N, 8, 1, Q))) * rng.random((N, 8, 16, Q))), 255)
    y = np.where(rng.random((N, 8, 1, Q)) < 0.5, 255 - y, y)
    L = np.minimum(np.floor(W * rng.random((N, 8, 16, Q)) ** 3), W - 1)
    C = np.where(C >= 0, W - 1 - np.minimum(np.floor(W * rng.random((N, 8, 16, Q)) ** 3), W - 1), -1)
    o = np.minimum(np.floor(16 * rng.random((N, 8, 16, Q)) ** 2), 15); b = rng.integers(0, 8, (N, 8, 16, Q))
    return pack(p, y, L, C, o, b, lim)
def setup_inputs_ends(rng):
    p = 255 * (rng.random((N, 8, 16, W)) < rng.choice(np.array([0.0, 0.5, 1.0]), (N, 8, 1, W))).astype(np.int64)
    y = 255 * (rng.random((N, 8, 16, Q)) < rng.choice(np.array([0.0, 0.5, 1.0]), (N, 8, 1, Q))).astype(np.int64)
    just = np.argsort(rng.random((N, 8, 16, Q)), axis=2) < 16 - M
    y = np.where(rng.random((N, 8, 1, Q)) < 0.25, 255 * just, y)
    L = (W - 1) * rng.integers(0, 2, (N, 8, 16, Q)); share = rng.choice(np.array([0.0, 0.5, 1.0]), (N, 8, 1, Q))
    C = np.where(rng.random((N, 8, 16, Q)) < share, W - 1, -1)
    o = 15 * rng.integers(0, 2, (N, 8, 16, Q)); b = 7 * rng.integers(0, 2, (N, 8, 16, Q)); lim = 3 * rng.integers(0, 2, (N, 8, 16, TV))
    turn = int(rng.integers(0, 4))
    for r in range(N):
        for g in range(8):
            w = (r + g + turn) % 4
            if (r, g) in ((0, 0), (N - 1, 7)): w = 3
            if (r, g) in ((0, 7), (N - 1, 6)): w = 1
            pm = rng.permutation(16)
            p[r, g, :, 0] = (0 * pm, 0 * pm + 255, 255 * (pm < M), 0 * pm)[w]
            p[r, g, :, W - 1] = (0 * pm + 255, 0 * pm, 255 * (pm < M - 1), 0 * pm)[w]
            for c in (0, Q - 1):
                if w == 3: y[r, g, :, c] = 255
                if w == 1:
                    y[r, g, :, c] = 0; L[r, g, :, c] = W - 1; L[r, g, 15, c] = 0; C[r, g, :, c] = W - 1; C[r, g, 15, c] = -1
                if w == 0:
                    y[r, g, :, c] = 254 + (pm < 16 - M); L[r, g, :, c] = 0; L[r, g, 15, c] = W - 1; C[r, g, :, c] = 0
    return pack(p, y, L, C, o, b, lim)
def setup_inputs_corners(rng):
    p, y, L, C, o, b, lim = parts(rng)
    p[..., :W // 4] = np.floor(0.125 * p[..., :W // 4]); p[..., W // 2:] = 96 + np.floor(160 * rng.random((N, 8, 16, W - W // 2))); p[..., W - 1] = 255
    y = 32 + np.floor(224 * rng.random((N, 8, 16, Q))); y = np.where(rng.random((N, 8, 1, Q)) < 0.125, 255, y)
    e = (np.arange(Q).reshape(1, 1, 1, Q) + rng.integers(0, 6, (N, 8, 1, 1))) % 6; k = np.arange(16).reshape(1, 1, 16, 1)
    name = np.where(rng.random((N, 8, 1, Q)) < 0.6, rng.integers(0, W // 4, (N, 8, 16, Q)), rng.integers(0, W, (N, 8, 16, Q)))
    hole = rng.choice(np.array([0, 15, 15, 6]), (N, 8, 1, Q))
    has = np.where(e == 0, False, np.where(e == 2, k != hole, np.where(e == 3, k == 15, True)))
    C = np.where(has, name, -1)
    L = np.where(rng.random((N, 8, 1, Q)) < 0.5, rng.integers(W // 2, W, (N, 8, 16, Q)), L)
    mode = rng.integers(0, 4, (N, 8, 1, Q)); o = np.where(mode == 0, k, np.where(mode == 1, 0, np.where(mode == 2, 15, o)))
    b = rng.choice(np.array([0, 0, 1, 3, 6, 7]), (N, 8, 16, Q)); b = np.where(e == 4, 7, np.where(e == 5, 7 * (k == 15), b))
    lim = 3 * rng.integers(0, 2, (N, 8, 16, TV))
    for c in (Q - 2, Q - 1):
        y[:, :, :, c] = 0; C[:, :, :, c] = -1; C[:, :, 15, c] = W - 1; b[:, :, 15, c] = 0
    y[:, 0, :, Q - 2] = 255; C[:, 0, :, Q - 2] = -1
    return pack(p, y, L, C, o, b, lim)
def setup_inputs_ties(rng):
    p, y, L, C, o, b, lim = parts(rng)
    base = rng.integers(2, 254, (1, 8, 16, 1))
    m = np.where(rng.random((N, 8, 1, W)) < 0.06, M + rng.integers(0, 2, (N, 8, 1, W)), rng.choice(np.array([M - 1, M - 1, M - 2, 0]), (N, 8, 1, W)))
    up = np.argsort(rng.random((N, 8, 16, W)), axis=2) < m
    p = base + np.where(m == 0, 0, np.where(up, 1, 0 - rng.integers(0, 2, (N, 8, 16, W))))
    y = base + np.where(rng.random((N, 8, 1, Q)) < 0.6, 0, rng.integers(-1, 2, (N, 8, 16, Q)))
    b = rng.integers(0, 3, (N, 8, 16, Q))
    p[..., :80] = (np.arange(80).reshape(1, 80) + np.arange(16).reshape(16, 1)) >> 4
    y[..., Q - 16:] = 255; L[..., Q - 16:] = rng.integers(0, 80, (N, 8, 16, 16)); L[..., Q - 8:] = rng.integers(0, 2, (N, 8, 16, 8))
    L[:, :, 0, Q - 16:] = 0; L[:, :, 15, Q - 8:] = 1
    us = np.arange(2048, 4081 - M).reshape(-1, 1); names = np.arange(2048, W).reshape(1, -1); x = us * names
    iu, ia = np.nonzero(((x & 63) == 32) & (x > 2 ** 23) & ((((x >> 5) + names + 97) & 255) == 0) & ((names & 255) < Q - 16))
    if len(iu) > 0:
        for g in range(8):
            s = int(rng.integers(0, len(iu))); u = int(us[iu[s], 0]); a = int(names[0, ia[s]]); c = a & 255
            p[:, g, :, a] = 255; y[:, g, :, c] = (u + np.argsort(rng.random((N, 16)), axis=1)) >> 4
            C[:, g, :, c] = -1; C[:, g, 0, c] = a; o[:, g, 0, c] = 0; b[:, g, 0, c] = 7
    return pack(p, y, L, C, o, b, lim)
def setup_inputs_alike(rng):
    p, y, L, C, o, b, lim = parts(rng); c = np.arange(Q).reshape(1, 1, 1, Q)
    few = np.array([0, W - 1, W // 2, 3])
    L[:, 0::4] = rng.choice(few, (N, 2, 16, Q))
    L[:, 1::4] = np.repeat(L[:, 1::4, :1], 16, axis=2)
    L[:, 2::4] = 256 * rng.integers(0, W // 256, (N, 2, 16, Q)) + c
    L[:, 3::4] = 256 * rng.integers(0, W // 256, (N, 2, 16, Q)) + (c + 1) % Q
    own = rng.random((N, 8, 1, Q)) < 0.5
    C = np.where((C >= 0) & own, L[:, :, ::-1], C); b[:, ::2] = 2
    return pack(p, y, L, C, o, b, lim)
def check_inputs(d):
    bad = []
    for k, lo, hi in (("prop", 0, 255), ("lem", 0, W - 1), ("con", -1, W - 1), ("org", 0, 15), ("cnt", 0, 7), ("ex", 0, 255), ("lim", 0, 3)):
        a = np.asarray(d[k]).astype(np.float64)
        if not (np.min(a) >= lo and np.max(a) <= hi): bad.append("range of " + k)
        elif not np.all(a == np.floor(a)): bad.append("whole numbers in " + k)
    return bad
def pick(p, a):
    return np.take_along_axis(p, a.reshape(N, 8, 1, 16 * Q), 3).reshape(N, 8, 16, 16, Q)
def at(a, k):
    return np.take_along_axis(a, k[:, :, None, :], 2)[:, :, 0]
def reference(prop, lem, con, org, cnt, ex, lim):
    p = prop.astype(np.float32).astype(np.int16).reshape(N, 8, 16, W); y = ex.astype(np.float32).astype(np.int16).reshape(N, 8, 16, Q)
    L = lem.astype(np.int64).reshape(N, 8, 16, Q); C = con.astype(np.int64).reshape(N, 8, 16, Q)
    o = org.astype(np.float32).astype(np.int64).reshape(N, 8, 16, Q); b = cnt.astype(np.float32).astype(np.int64).reshape(N, 8, 16, Q)
    lm = lim.astype(np.int64).reshape(N, 8, 16, TV); w = np.zeros((N, Q), np.int64)
    rows = np.arange(16).reshape(1, 1, 16, 1); lane = np.arange(Q).reshape(1, 1, Q)
    for t in range(TV):
        y5 = y[:, :, :, None, :]; pl = pick(p, L); pc = pick(p, np.maximum(C, 0))
        bar = (np.add.reduce(pc > y5, axis=2, dtype=np.int64) >= M) & (C >= 0)
        gui = np.add.reduce(pl > y5, axis=2, dtype=np.int64) >= M
        score = np.add.reduce(np.abs(pl - y5), axis=2, dtype=np.int64); u = np.add.reduce(y, axis=2, dtype=np.int64)
        barred = np.any(bar, axis=2); some = np.any(gui, axis=2); guilty = ~barred & some; clear = ~barred & ~some
        kb = np.argmax(bar, axis=2); hit = barred[:, :, None] & (rows == kb[:, :, None]); b1 = b + hit
        over = hit & (b1 > lm[:, :, :, t:t + 1] + w[:, None, None, :]); back = np.any(over, axis=2)
        L1 = np.where(back[:, :, None] & (rows == at(o, kb)[:, :, None]), at(C, kb)[:, :, None], L)
        C1 = np.where(over, -1, C); b1 = np.where(over, 0, b1)
        kg = np.argmax(gui, axis=2); old = at(L, kg); empty = C < 0
        slot = np.where(np.any(empty, axis=2), np.argmax(empty, axis=2), np.argmax(b, axis=2)); put = guilty[:, :, None] & (rows == slot[:, :, None])
        n = ((((u * old) >> 5) + old + 97 * t) & (W - 256)) + lane
        C1 = np.where(put, old[:, :, None], C1); o1 = np.where(put, kg[:, :, None], o); b1 = np.where(put, 0, b1)
        L1 = np.where(guilty[:, :, None] & (rows == kg[:, :, None]), n[:, :, None], L1)
        pv = np.take_along_axis(pl, kg[:, :, None, None, :], 3)[:, :, :, 0]
        np.put_along_axis(p, n[:, :, None, :], np.where(guilty[:, :, None], np.minimum(pv, y), np.take_along_axis(p, n[:, :, None, :], 3)), 3)
        y = np.where(guilty[:, :, None], np.abs(y - pv), y)
        ks = np.argmin(score, axis=2); new = (((u * u) >> 5) + 37 * u + t) & (W - 1)
        L1 = np.where(clear[:, :, None] & (rows == ks[:, :, None]), new[:, :, None], L1)
        w = np.add.reduce(barred, axis=1, dtype=np.int64) & 3
        L, C, o, b = L1, C1, o1, b1
        if t < TV - 1: L, C, o, b = [np.roll(a, HOP, axis=0) for a in (L, C, o, b)]
    def half(a): return a.reshape(N, 128, -1).astype(np.float32).astype(BF)
    return {"zp": half(p), "zl": L.reshape(N, 128, Q).astype(np.float32), "zc": C.reshape(N, 128, Q).astype(np.float32), "zo": half(o), "zb": half(b), "zy": half(y)}

@@ -1,0 +1,471 @@
+from concourse.mybir import dt, AluOpType, AxisListType, ActivationFunctionType
+
+N, W, Q, TV, HOP = 8, 4096, 192, 6, 3
+NPOS = 16 * Q
+CH = 3
+PW = 4608
+DUMP = 4352
+
+SCRATCH = {
+    "P": ("sbuf", [128, PW], "bfloat16"),
+    "D": ("sbuf", [128, NPOS + Q], "bfloat16"),
+    "AB0": ("sbuf", [128, NPOS + Q], "bfloat16"),
+    "AB1": ("sbuf", [128, NPOS + Q], "bfloat16"),
+    "SG": ("sbuf", [128, NPOS], "bfloat16"),
+    "IC": ("sbuf", [128, NPOS], "bfloat16"),
+    "YE": ("sbuf", [128, NPOS], "bfloat16"),
+    "YL": ("sbuf", [128, Q], "uint16"),
+    "inL": ("sbuf", [128, Q], "int32"), "inC": ("sbuf", [128, Q], "int32"),
+    "inO": ("sbuf", [128, Q], "bfloat16"), "inB": ("sbuf", [128, Q], "bfloat16"),
+    "inLim": ("sbuf", [128, 8], "int32"), "limF": ("sbuf", [128, 8], "float32"),
+    "MSK": ("sbuf", [128, Q], "float32"), "RSTL": ("sbuf", [128, Q], "float32"), "RSTC": ("sbuf", [128, Q], "float32"),
+    "KT": ("sbuf", [128, Q], "bfloat16"), "CL": ("sbuf", [128, Q], "bfloat16"), "CC": ("sbuf", [128, Q], "bfloat16"),
+    "ONE": ("sbuf", [128, 128], "bfloat16"),
+    "Z1": ("sbuf", [128, 144], "bfloat16"), "ZL": ("sbuf", [128, 144], "bfloat16"), "ZC": ("sbuf", [128, 144], "bfloat16"), "ZS": ("sbuf", [128, 144], "bfloat16"),
+    "GW": ("sbuf", [128, 128], "bfloat16"), "BO": ("sbuf", [128, 128], "bfloat16"),
+    "PM": ("sbuf", [128, Q], "bfloat16"), "PM1": ("sbuf", [128, Q], "bfloat16"),
+    "S00": ("sbuf", [128, 128], "float32"), "S01": ("sbuf", [128, 128], "float32"), "S10": ("sbuf", [128, 128], "float32"), "S11": ("sbuf", [128, 128], "float32"),
+    "CM1": ("sbuf", [128, 384], "float32"),
+    "pI": ("sbuf", [128, Q], "int32"), "qI": ("sbuf", [128, Q], "int32"), "gI": ("sbuf", [128, Q], "int32"),
+    "nI": ("sbuf", [128, 144], "int32"), "mpI": ("sbuf", [128, 128], "int32"), "tI": ("sbuf", [128, Q], "int32"), "tI2": ("sbuf", [128, Q], "int32"), "c16I": ("sbuf", [128, Q], "int32"),
+    "b4": ("sbuf", [128, 8], "int32"), "b0F": ("sbuf", [128, 8], "float32"), "b1F": ("sbuf", [128, 8], "float32"),
+    "cF": ("sbuf", [128, 48], "float32"), "c256": ("sbuf", [128, 12], "int32"),
+    "X0": ("sbuf", [128, 384], "float32"), "X1": ("sbuf", [128, 384], "float32"),
+    "T0": ("sbuf", [128, 416], "float32"), "T1": ("sbuf", [128, 416], "float32"), "E0": ("sbuf", [128, 384], "float32"),
+    "tA": ("sbuf", [128, Q], "float32"), "tB": ("sbuf", [128, Q], "float32"), "tC": ("sbuf", [128, Q], "float32"), "tD": ("sbuf", [128, Q], "float32"),
+    "oB": ("sbuf", [128, 384], "bfloat16"),
+    "y_": ("sbuf", [128, Q], "float32"), "KEYC": ("sbuf", [128, Q], "float32"), "SLT": ("sbuf", [128, Q], "float32"), "tS": ("sbuf", [128, Q], "int32"),
+    "mkL": ("sbuf", [128, Q], "float32"), "mk": ("sbuf", [128, Q], "float32"), "hot": ("sbuf", [128, Q], "float32"),
+    "RL": ("sbuf", [128, Q], "float32"), "RS": ("sbuf", [128, Q], "float32"), "RC": ("sbuf", [128, Q], "float32"),
+    "bL": ("sbuf", [128, Q], "float32"), "bR": ("sbuf", [128, Q], "float32"), "bN": ("sbuf", [128, Q], "float32"),
+    "dif": ("sbuf", [128, Q], "float32"), "sL": ("sbuf", [128, Q], "int32"), "sM": ("sbuf", [128, Q], "int32"), "sC": ("sbuf", [128, Q], "int32"),
+    "LI": ("sbuf", [128, 320], "int32"), "LF": ("sbuf", [128, 480], "float32"), "Bf": ("sbuf", [128, 12], "bfloat16"),
+    "LST": ("sbuf", [128, 24], "uint16"),
+    "md": ("sbuf", [128, Q], "bfloat16"), "nD": ("sbuf", [128, Q], "bfloat16"),
+    "XL": ("psum", [128, 512], "float32"), "XS": ("psum", [128, 512], "float32"), "XC": ("psum", [128, 512], "float32"),
+    "VP1": ("psum", [128, 512], "float32"), "VP2": ("psum", [128, 512], "float32"), "VT": ("psum", [128, 512], "float32"),
+    "MI": ("psum", [128, 512], "float32"), "SWP": ("psum", [128, 512], "float32"),
+}
+PART = {"cv": ("cF", 0, 12), "cp": ("cF", 12, 12), "cb": ("cF", 24, 24), "us": ("LF", 372, 12), "wI": ("LI", 252, 24)}
+for _t in range(TV):
+    SCRATCH["DL%d" % _t] = ("sbuf", [128, Q], "float32")
+    SCRATCH["oL%d" % _t] = ("sbuf", [128, Q], "uint16")
+    SCRATCH["oC%d" % _t] = ("sbuf", [128, Q], "uint16")
+    SCRATCH["oV%d" % _t] = ("sbuf", [128, 2 * Q], "int32")
+    if _t:
+        SCRATCH["aL%d" % _t] = ("sbuf", [128, Q], "uint16")
+        SCRATCH["aC%d" % _t] = ("sbuf", [128, Q], "uint16")
+        SCRATCH["aV%d" % _t] = ("sbuf", [128, 2 * Q], "int32")
+SEMAPHORES = ["sv", "ss", "st", "sg", "snt"] + ["d%d" % i for i in range(16)] + [k + "%d" % t for k in ("qL", "qC", "qV") for t in range(1, TV)]
+
+
+def rank_program(g, core, T, topo):
+    rank = T.rank_of(core)
+    if rank is None:
+        return
+    dst = T.cores[(rank + HOP) % N]
+    rid, pid = topo.addr(dst)[:2]
+    emask = topo.mask(core, dst)
+    neng = len(topo.engines(core, dst))
+    op = AluOpType
+    af = ActivationFunctionType
+    queues = {"v": g.vector, "s": g.scalar, "t": g.tensor, "g": g, "y": g.sync}
+    semof = {"v": "sv", "s": "ss", "t": "st", "g": "sg"}
+    count = {}
+    clock = {e: {} for e in queues}
+    wr, rd = {}, {}
+    psum = {k for k in SCRATCH if SCRATCH[k][0] == "psum"}
+
+    def A(name, lo=0, hi=None, st=1):
+        if name in PART:
+            name, base, n = PART[name]
+            lo, hi = base + lo, base + (n if hi is None else hi)
+        hi = SCRATCH[name][1][1] if hi is None else hi
+        return (name, lo, hi, T[name][:, lo:hi] if st == 1 else T[name][:, lo:hi:st])
+
+    def emit(e, fn, R, Wt, sem=None, inc=1):
+        need = []
+        for (nm, lo, hi, _) in R:
+            for (l, h, o) in wr.get(nm, []):
+                if (l < hi and lo < h) or (nm in psum and o["e"] != e):
+                    need.append(o)
+            if nm in psum:
+                need += [o for (l, h, o) in rd.get(nm, []) if o["e"] != e]
+        for (nm, lo, hi, _) in Wt:
+            for (l, h, o) in wr.get(nm, []):
+                if (l < hi and lo < h) or (nm in psum and o["e"] != e):
+                    need.append(o)
+            for (l, h, o) in rd.get(nm, []):
+                if (l < hi and lo < h) or (nm in psum and o["e"] != e):
+                    need.append(o)
+        want = {}
+        for o in need:
+            if o["v"] > want.get(o["s"], (0, None))[0]:
+                want[o["s"]] = (o["v"], o)
+        ck = clock[e]
+        for s in sorted(want, key=lambda s: -len(want[s][1]["c"])):
+            v, o = want[s]
+            if ck.get(s, 0) >= v:
+                continue
+            queues[e].wait_ge(T.sem[s], v)
+            for k, x in o["c"].items():
+                ck[k] = max(ck.get(k, 0), x)
+            ck[s] = max(ck.get(s, 0), v)
+        ins = fn(queues[e])
+        s = sem or semof[e]
+        if inc:
+            ins.then_inc(T.sem[s], inc)
+            count[s] = count.get(s, 0) + inc
+        me = {"e": "dma" if inc == 16 else e, "s": s, "v": count.get(s, 0), "c": dict(ck)}
+        for (nm, lo, hi, _) in R:
+            rd.setdefault(nm, []).append((lo, hi, me))
+        for (nm, lo, hi, a) in Wt:
+            wr[nm] = [x for x in wr.get(nm, []) if not (lo <= x[0] and x[1] <= hi)] + [(lo, hi, me)]
+            rd[nm] = [x for x in rd.get(nm, []) if not (lo <= x[0] and x[1] <= hi) or x[2] is me]
+        return me
+
+    def ts(o, i, s1, op0, s2=None, op1=None):
+        if op1 is None:
+            emit("v", lambda q: q.tensor_scalar(o[3], i[3], s1, None, op0), [i], [o])
+        else:
+            sc = s2[3] if isinstance(s2, tuple) else s2
+            emit("v", lambda q: q.tensor_scalar(o[3], i[3], s1, sc, op0, op1), [i] + ([s2] if isinstance(s2, tuple) else []), [o])
+
+    def tt(o, a, b, o_):
+        emit("v", lambda q: q.tensor_tensor(o[3], a[3], b[3], o_), [a, b], [o])
+
+    def cp(o, i):
+        emit("v", lambda q: q.tensor_copy(o[3], i[3]), [i], [o])
+
+    def fill(o, c):
+        emit("v", lambda q: q.memset(o[3], c), [], [o])
+
+    def scan(o, d0, d1, init, p0, p1):
+        emit("v", lambda q: q.tensor_tensor_scan(o[3], d0[3], d1[3], init, p0, p1), [d0, d1], [o])
+
+    def act(o, i, f, bias=0.0, scale=1.0, off=None):
+        src = i[3].indirect(off[3]) if off else i[3]
+        emit("s", lambda q: q.activation(o[3], src, f, bias=bias, scale=scale), [i] + ([off] if off else []), [o])
+
+    def iota(o, pattern, base, cm):
+        emit("g", lambda q: q.iota(o[3], pattern, base, cm), [], [o])
+
+    def mms(o, terms):
+        R = [x for t in terms for x in t]
+
+        def go(q):
+            for j, (l, r) in enumerate(terms):
+                ins = q.matmul(o[3], l[3], r[3], j == 0, j == len(terms) - 1)
+            return ins
+        emit("t", go, R, [o])
+
+    nd = [0]
+
+    def dma(e, o, i, R=[], Wt=[]):
+        emit(e, lambda q: q.dma_start(o, i), R, Wt, sem="d%d" % nd[0], inc=16)
+        nd[0] += 1
+
+    def load(e, o, src):
+        dma(e, o[3], src, [], [o])
+
+    def LI(j):
+        return A("LI", 12 * j, 12 * j + 12)
+
+    def LF(j):
+        return A("LF", 12 * j, 12 * j + 12)
+
+    load("y", A("inL"), T.lem[:, :])
+    load("s", A("inC"), T.con[:, :])
+    load("y", A("inO"), T.org[:, :])
+    load("s", A("inB"), T.cnt[:, :])
+    load("y", A("inLim", 0, TV), T.lim[:, :])
+    load("s", A("AB0", NPOS, NPOS + Q), T.ex[:, :])
+    load("y", A("P", 0, W), T.prop[:, :])
+
+    iota(A("pI"), [[0, Q]], 0, 1)
+    iota(A("mpI"), [[1, 128]], 0, -1)
+    iota(A("gI"), [[0, 12], [1, 16]], 0, 0)
+    iota(A("nI"), [[1, 144]], 0, 0)
+    iota(A("c16I"), [[16, 12], [0, 16]], 0, 0)
+    emit("g", lambda q: q.iota(T.CM1[:, :], [[0, 12], [1, 2], [0, 16]], 0, 0, allow_small_or_imprecise_dtypes=True), [], [A("CM1")])
+    iota(A("c256"), [[256, 12]], 0, 0)
+    kI = A("gI")
+    fill(A("T0", 0, 16), 0.0); fill(A("T0", 400, 416), 0.0); fill(A("T1", 0, 16), 0.0); fill(A("T1", 400, 416), 0.0)
+    ts(A("b4", 0, 1), A("pI", 0, 1), 16, op.bitwise_and)
+    ts(A("b0F", 0, 1), A("b4", 0, 1), 0, op.is_equal)
+    ts(A("b1F", 0, 1), A("b4", 0, 1), 16, op.is_equal)
+    ts(A("S00"), A("mpI"), 0, op.is_equal, A("b0F", 0, 1), op.mult)
+    ts(A("S11"), A("mpI"), 0, op.is_equal, A("b1F", 0, 1), op.mult)
+    ts(A("S01"), A("mpI"), 16, op.is_equal, A("b0F", 0, 1), op.mult)
+    ts(A("S10"), A("mpI"), -16, op.is_equal, A("b1F", 0, 1), op.mult)
+
+    def swap(x):
+        tt(A("T1", 16, 400), x, A("CM1"), op.mult)
+        tt(A("T0", 16, 400), x, A("T1", 16, 400), op.subtract)
+        mms(A("SWP", 0, 384), [(A("S00"), A("T0", 16, 400)), (A("S11"), A("T1", 16, 400)), (A("S01"), A("T1", 32, 416)), (A("S10"), A("T0", 0, 384))])
+
+    def vtr(o, i):
+        emit("v", lambda q: q.transpose(o[3], i[3]), [i], [o])
+    cp(A("X0", 0, Q), A("inL"))
+    ts(A("tA"), A("inO"), -16384, op.mult, 15 * 16384, op.add)
+    ts(A("tB"), A("inC"), 0, op.max, 2, op.mult)
+    tt(A("tA"), A("tA"), A("tB"), op.add)
+    ts(A("tB"), A("inB"), 1 << 18, op.mult)
+    tt(A("tA"), A("tA"), A("tB"), op.add)
+    ts(A("tC"), A("inB"), 2 - (1 << 18), op.mult, (1 << 21) + (1 << 13), op.add)
+    ts(A("tD"), A("inC"), 0, op.is_lt)
+    tt(A("tC"), A("tC"), A("tD"), op.mult)
+    tt(A("X0", Q, 2 * Q), A("tA"), A("tC"), op.add)
+    vtr(A("X1"), A("X0"))
+    swap(A("X1"))
+    K13, K21 = A("VP1", 0, Q), A("VP1", Q, 2 * Q)
+    KC, TH = A("VP2", 0, Q), A("VP2", Q, 2 * Q)
+    TA, TB = A("VT", 0, Q), A("VT", Q, 2 * Q)
+    ts(K13, kI, -8192, op.mult, 4096 + 15 * 8192, op.add)
+    cp(A("oL0"), A("SWP", 0, Q))
+    cp(A("oV0", Q, 2 * Q), A("SWP", Q, 2 * Q))
+    cp(A("tA"), A("SWP", 0, Q))
+    tt(A("oV0", 0, Q), A("tA"), K13, op.add)
+
+    def coff(t):
+        ts(A("sC"), A("oV%d" % t, Q, 2 * Q), 1, op.arith_shift_right, 8191, op.bitwise_and)
+        cp(A("oC%d" % t), A("sC"))
+    coff(0)
+    ts(A("qI"), A("pI"), 15, op.bitwise_and)
+    tt(A("tI"), A("c16I"), A("qI"), op.add)
+    cp(A("YL"), A("tI"))
+    fill(A("P", W, PW), 0.0)
+    fill(A("D", NPOS, NPOS + Q), 0.0)
+
+    def yexp(p):
+        n = Q // CH
+        for c in range(CH):
+            act(A("YE", c * NPOS // CH, (c + 1) * NPOS // CH), A("AB%d" % p, NPOS, NPOS + Q), af.Copy, off=A("YL", c * n, (c + 1) * n))
+    yexp(0)
+    ts(A("tI", 0, 144), A("pI", 0, 144), 240, op.bitwise_and)
+    tt(A("tI2", 0, 144), A("nI"), A("tI", 0, 144), op.subtract)
+    for z, s in (("ZL", 2.0 ** 25), ("ZS", -16.0), ("ZC", 2.0 ** 26), ("Z1", 1.0)):
+        ts(A(z), A("tI2", 0, 144), 15, op.is_equal, s, op.mult)
+    fill(A("ONE"), 1.0 / 128)
+    fill(A("CL"), 2.0 ** 25)
+    fill(A("CC"), -7.5 * 2.0 ** 26)
+    ts(A("KT"), kI, -1, op.mult, 15, op.add)
+    ts(A("MSK"), kI, 0, op.is_gt)
+
+    def gather_l(t):
+        n = Q // CH
+        lst = ("aL%d" if t else "oL%d") % t
+        for c in range(CH):
+            lo, hi = c * NPOS // CH, (c + 1) * NPOS // CH
+            off, ye, o = A(lst, c * n, (c + 1) * n), A("YE", lo, hi), A("D", lo, hi)
+            emit("v", lambda q: q.tensor_tensor(o[3], T.P[:, :].indirect(off[3]), ye[3], op.subtract), [A("P"), off, ye], [o])
+            act(A("SG", lo, hi), o, af.Sign, bias=-0.5)
+            act(A("AB%d" % (t % 2), lo, hi), o, af.Abs)
+            cnt("XL", "SG", "ZL", "CL", c)
+            cnt("XS", "AB%d" % (t % 2), "ZS", "KT", c)
+
+    def gather_c(t):
+        n = Q // CH
+        lst = ("aC%d" if t else "oC%d") % t
+        for c in range(CH):
+            lo, hi = c * NPOS // CH, (c + 1) * NPOS // CH
+            off, ye, o = A(lst, c * n, (c + 1) * n), A("YE", lo, hi), A("IC", lo, hi)
+            emit("v", lambda q: q.tensor_tensor(o[3], T.P[:, :].indirect(off[3]), ye[3], op.is_gt), [A("P"), off, ye], [o])
+            cnt("XC", "IC", "ZC", "CC", c)
+
+    def cnt(x, src, z, const, c):
+        n = Q // CH
+        mms(A(x, c * n, (c + 1) * n), [(A("ONE"), A(const, c * n, (c + 1) * n))] +
+            [(A(z, 15 - q, 143 - q), A(src, c * n * 16 + q, (c + 1) * n * 16, 16)) for q in range(16)])
+
+    def usum(p):
+        mms(A("MI", 0, 12), [(A("Z1", 15 - q, 143 - q), A("AB%d" % p, NPOS + q, NPOS + Q, 16)) for q in range(16)])
+        act(A("us"), A("MI", 0, 12), af.Copy)
+
+    gather_l(0)
+    ts(K21, kI, -(1 << 21), op.mult, 15 * (1 << 21) - (1 << 24) + (1 << 13), op.add)
+    ts(KC, kI, -2, op.mult, 30 - (1 << 24) - (1 << 13), op.add)
+    ts(A("RSTL"), A("MSK"), 2.0 ** 27, op.mult, -2.0 ** 20, op.add)
+    ts(A("RSTC"), A("MSK"), 2.0 ** 28, op.mult, -2.0 ** 27, op.add)
+    cp(A("limF", 0, TV), A("inLim", 0, TV))
+    tt(A("tI"), kI, A("qI"), op.subtract)
+    ts(A("tA"), A("tI"), 0, op.is_equal)
+    ts(A("tB"), A("tI"), 1, op.is_equal)
+    tt(A("PM"), A("tA"), A("tB"), op.subtract)
+    ts(A("tI2", 0, 128), A("nI", 0, 128), 240, op.bitwise_and)
+    ts(A("tI", 0, 128), A("pI", 0, 128), 240, op.bitwise_and)
+    tt(A("BO"), A("tI2", 0, 128), A("tI", 0, 128), op.is_equal)
+    ts(A("tI", 0, 128), A("mpI"), 15, op.bitwise_and)
+    ts(A("GW"), A("tI", 0, 128), 0, op.is_equal)
+    tt(A("tI", 0, 12), A("c16I", 0, Q, 16), A("qI", 0, 12), op.add)
+    cp(A("cv"), A("tI", 0, 12))
+    ts(A("cb", 0, 12), A("cv"), NPOS, op.add)
+    ts(A("cb", 12, 24), A("cv"), DUMP, op.add)
+    tt(A("cp"), A("c256"), A("qI", 0, 12), op.add)
+    ts(A("cp"), A("cp"), 240, op.add)
+    tt(A("cp"), A("cp"), A("cb", 0, 12), op.subtract)
+    fill(A("bL"), 0.0); fill(A("bR"), 0.0); fill(A("bN"), 0.0)
+    usum(0)
+
+    def lims(t):
+        ts(A("PM1"), A("PM"), A("limF", t, t + 1)[3], op.mult)
+        mms(A("SWP", 0, Q), [(A("BO"), A("PM1"))])
+        act(A("DL%d" % t), A("SWP", 0, Q), af.Copy, scale=2.0 ** 18)
+
+    def starts(name, a=15):
+        return A(name, a, Q, 16)
+
+    for t in range(TV):
+        p = t % 2
+        AB, yv = A("AB%d" % p), A("AB%d" % p, NPOS, NPOS + Q)
+        if t:
+            gather_l(t)
+        pv = ("aV%d" if t else "oV%d") % t
+        Lp, V = A(pv, 0, Q), A(pv, Q, 2 * Q)
+        if t == 0:
+            lims(0)
+            scan(TH, A("MSK"), A("DL0"), 0.0, op.mult, op.add)
+        gather_c(t)
+        tt(TA, V, TH, op.is_ge)
+        tt(A("y_"), TA, V, op.add)
+        ts(A("tS"), V, 15 << 18, op.bitwise_and, 9, op.arith_shift_right)
+        tt(A("KEYC"), A("y_"), K21, op.add)
+        tt(A("SLT"), A("tS"), KC, op.add)
+        tt(A("mkL"), A("XL", 0, Q), Lp, op.min)
+        scan(A("RS"), A("RSTL"), A("XS", 0, Q), -2.0 ** 20, op.min, op.max)
+        scan(A("RL"), A("RSTL"), A("mkL"), -2.0 ** 20, op.min, op.max)
+        RL, RS, RC = starts("RL"), starts("RS"), starts("RC")
+        cp(LI(0), RL)
+        cp(LI(1), RS)
+        tt(LI(10), A("us"), A("us"), op.mult)
+        ts(LI(2), LI(0), 4095, op.bitwise_and)
+        ts(LI(11), LI(10), 5, op.arith_shift_right)
+        tt(LI(3), LI(2), A("us"), op.mult)
+        ts(LF(0), A("us"), 37, op.mult, t, op.add)
+        ts(LI(4), LI(3), 5, op.arith_shift_right)
+        tt(LI(12), LI(11), LF(0), op.add)
+        tt(LI(5), LI(4), LI(2), op.add)
+        ts(LI(13), LI(12), 4095, op.bitwise_and)
+        if t:
+            ts(LI(6), LI(5), 97 * t, op.add)
+        ts(LI(14), LI(1), 15, op.bitwise_and)
+        ts(LI(7), LI(6 if t else 5), 3840, op.bitwise_and)
+        ts(LF(1), LI(14), 8192, op.mult, 4096, op.add)
+        tt(LF(2), A("cv"), LI(2), op.subtract)
+        tt(LF(3), LF(1), LI(13), op.add)
+        tt(LF(4), LI(7), LF(2), op.add)
+        ts(LF(5), RL, 0, op.is_lt)
+        tt(LF(6), LF(4), RL, op.add)
+        tt(LF(7), LF(5), LF(3), op.mult)
+        ts(LF(8), RL, 0, op.is_ge)
+        tt(LF(9), LF(6), LF(7), op.max)
+        ts(LI(15), LI(0), 9, op.arith_shift_right, 240, op.bitwise_and)
+        ts(LF(10), RL, 2, op.mult, -8192, op.add)
+        tt(LF(11), A("cp"), LI(15), op.subtract)
+        ts(LF(12), LI(7), -DUMP, op.add)
+        tt(TA, A("XC", 0, Q), A("KEYC"), op.min)
+        tt(A("mk"), TA, A("SLT"), op.max)
+        scan(A("RC"), A("RSTC"), A("mk"), -2.0 ** 27, op.min, op.max)
+        cp(LI(16), RC)
+        ts(LF(13), RC, -2.0 ** 24, op.is_lt)
+        ts(LI(17), LI(16), 1, op.bitwise_and)
+        ts(LI(18), LI(16), 0x3FFFE, op.bitwise_and, 1, op.arith_shift_right)
+        tt(LF(14), LF(13), LF(9), op.mult)
+        tt(LF(15), LI(17), LI(18), op.mult)
+        ts(LI(19), LI(16), 0x1FDFFE, op.bitwise_and)
+        ts(LI(20), LI(16), 0x3C000, op.bitwise_and)
+        tt(starts("bL", 0), LF(14), LF(15), op.add)
+        tt(LF(16), LF(13), LF(8), op.mult)
+        scan(TA, A("MSK"), A("bL"), 0.0, op.mult, op.add)
+        tt(LF(18), LF(11), LF(16), op.mult)
+        tt(A("dif"), TA, Lp, op.subtract)
+        tt(LF(19), LF(12), LF(16), op.mult)
+        ts(TB, A("dif"), -4096, op.max, 4096, op.min)
+        ts(LF(17), RC, -2.0 ** 24, op.is_ge)
+        tt(A("sL"), TB, Lp, op.add)
+        tt(A("LF", 240, 264), A("LF", 216, 240), A("cb"), op.add)
+        ts(A("sM"), A("sL"), 4095, op.bitwise_and)
+        cp(A("LST"), A("LF", 240, 264))
+        nxt = t + 1
+        last = nxt == TV
+
+        def send(nm, k):
+            o, i = T["a%s%d" % (k, nxt)], T["o%s%d" % (k, nxt)]
+            emit("g", lambda q: q.remote_dma(out_ap=o[:, :], in_ap=i[:, :], remote_sem=T.sem["q%s%d" % (k, nxt)], local_sem=T.sem.snt,
+                                             pid=pid, routing_id=rid, dma_engine_mask=emask), [A("o%s%d" % (k, nxt))], [], inc=0)
+            count["snt"] = count.get("snt", 0) + neng
+            nm_ = "a%s%d" % (k, nxt)
+            wr[nm_] = [(0, SCRATCH[nm_][1][1], {"e": "net", "s": "q%s%d" % (k, nxt), "v": neng, "c": {}})]
+        if not last:
+            cp(A("oL%d" % nxt), A("sM"))
+            send("oL", "L")
+        PL, NL = A("LST", 0, 12), A("LST", 12, 24)
+        act(A("nD"), A("D"), af.Relu, scale=-1.0, off=PL)
+        act(A("md"), A("nD"), af.Copy, scale=-1.0)
+        act(A("AB%d" % (1 - p), NPOS, NPOS + Q), AB, af.Copy, off=PL)
+        tt(LF(21), LF(17), LF(8), op.max)
+        ts(LF(22), LI(19), 1 << 18, op.add)
+        tt(starts("bR", 0), LF(21), RC, op.mult)
+        ts(LF(23), LI(20), (1 << 21) + (1 << 13), op.add)
+        scan(TA, A("MSK"), A("bR"), 0.0, op.mult, op.add)
+        tt(LF(24), LF(23), LI(17), op.mult)
+        tt(LF(25), LF(22), LF(24), op.max)
+        tt(LF(26), LF(10), LF(13), op.mult)
+        tt(A("hot"), A("mk"), TA, op.is_equal)
+        tt(LF(27), LF(25), LF(17), op.mult)
+        tt(starts("bN", 0), LF(26), LF(27), op.add)
+        scan(TA, A("MSK"), A("bN"), 0.0, op.mult, op.add)
+        tt(TB, TA, V, op.subtract)
+        ov = "oV%d" % nxt if not last else "oV0"
+        tt(TA, A("hot"), TB, op.mult)
+        pnew = lambda: emit("v", lambda q: q.tensor_tensor(T.P[:, :].indirect(NL[3]), T.md[:, :], yv[3], op.add), [A("md"), yv, NL], [A("P")])
+        if last:
+            pnew()
+            tt(A(ov, Q, 2 * Q), TA, V, op.add)
+            break
+        tt(A(ov, Q, 2 * Q), TA, V, op.add)
+        coff(nxt)
+        send("oC", "C")
+        tt(A(ov, 0, Q), A("sM"), K13, op.add)
+        send("oV", "V")
+        yexp(1 - p)
+        pnew()
+        cp(A("Bf"), LF(17))
+        mms(A("MI", 0, 12), [(A("GW"), A("Bf"))])
+        cp(A("wI", 0, 12), A("MI", 0, 12))
+        ts(A("wI", 12, 24), A("wI", 0, 12), 3, op.bitwise_and)
+        ts(LF(30), A("wI", 12, 24), 1 << 18, op.mult)
+        lims(nxt)
+        d = "DL%d" % nxt
+        tt(starts(d, 0), starts(d, 0), LF(30), op.add)
+        scan(TH, A("MSK"), A(d), 0.0, op.mult, op.add)
+        usum(1 - p)
+
+    dma("y", T.zp[:, :], T.P[:, 0:W], [A("P", 0, W)])
+    dma("y", T.zy[:, :], T.AB0[:, NPOS:NPOS + Q], [A("AB0", NPOS, NPOS + Q)])
+    VN = A("oV0", Q, 2 * Q)
+    cp(A("X0", 0, Q), A("sM"))
+    ts(A("sL"), VN, 1, op.arith_shift_right, 8191, op.bitwise_and)
+    ts(A("tA"), A("sL"), 4096, op.is_lt)
+    ts(A("tB"), A("sL"), 1, op.add)
+    ts(A("sM"), VN, 14, op.arith_shift_right, 15, op.bitwise_and)
+    tt(A("tC"), A("tA"), A("tB"), op.mult)
+    ts(A("X0", Q, 2 * Q), A("tC"), -1, op.add)
+    ts(A("X1", 0, Q), A("sM"), -1, op.mult, 15, op.add)
+    ts(A("sC"), VN, 18, op.arith_shift_right, 7, op.bitwise_and)
+    ts(A("tB"), A("sL"), -4096, op.add, 0, op.max)
+    tt(A("X1", Q, 2 * Q), A("sC"), A("tB"), op.add)
+    swap(A("X0"))
+    cp(A("E0"), A("SWP", 0, 384))
+    swap(A("X1"))
+    vtr(A("X0"), A("E0"))
+    dma("y", T.zl[:, :], T.X0[:, 0:Q], [A("X0", 0, Q)])
+    dma("s", T.zc[:, :], T.X0[:, Q:2 * Q], [A("X0", Q, 2 * Q)])
+    cp(A("E0"), A("SWP", 0, 384))
+    vtr(A("X1"), A("E0"))
+    cp(A("oB"), A("X1"))
+    dma("y", T.zo[:, :], T.oB[:, 0:Q], [A("oB", 0, Q)])
+    dma("s", T.zb[:, :], T.oB[:, Q:2 * Q], [A("oB", Q, 2 * Q)])
+    for s in sorted(count):
+        if count[s] and clock["g"].get(s, 0) < count[s]:
+            g.wait_ge(T.sem[s], count[s])

@@ -1,62 +1,49 @@
-from concourse.mybir import dt, AluOpType, AxisListType, ActivationFunctionType
+from concourse.mybir import AluOpType, ActivationFunctionType
 
 N, W, Q, TV, HOP = 8, 4096, 192, 6, 3
 NPOS = 16 * Q
-CH = 3
 PW = 4608
 DUMP = 4352
+LCH = [(0, 64), (64, 128), (128, 192)]
+CCH = [(0, 64), (64, 128)]
+SCH = [(128, 160), (160, 192)]
 
-SCRATCH = {
-    "P": ("sbuf", [128, PW], "bfloat16"),
-    "D": ("sbuf", [128, NPOS + Q], "bfloat16"),
-    "AB0": ("sbuf", [128, NPOS + Q], "bfloat16"),
-    "AB1": ("sbuf", [128, NPOS + Q], "bfloat16"),
-    "SG": ("sbuf", [128, NPOS], "bfloat16"),
-    "IC": ("sbuf", [128, NPOS], "bfloat16"),
-    "YE": ("sbuf", [128, NPOS], "bfloat16"),
-    "YL": ("sbuf", [128, Q], "uint16"),
-    "inL": ("sbuf", [128, Q], "int32"), "inC": ("sbuf", [128, Q], "int32"),
-    "inO": ("sbuf", [128, Q], "bfloat16"), "inB": ("sbuf", [128, Q], "bfloat16"),
-    "inLim": ("sbuf", [128, 8], "int32"), "limF": ("sbuf", [128, 8], "float32"),
-    "MSK": ("sbuf", [128, Q], "float32"), "RSTL": ("sbuf", [128, Q], "float32"), "RSTC": ("sbuf", [128, Q], "float32"),
-    "KT": ("sbuf", [128, Q], "bfloat16"), "CL": ("sbuf", [128, Q], "bfloat16"), "CC": ("sbuf", [128, Q], "bfloat16"),
-    "ONE": ("sbuf", [128, 128], "bfloat16"),
-    "Z1": ("sbuf", [128, 144], "bfloat16"), "ZL": ("sbuf", [128, 144], "bfloat16"), "ZC": ("sbuf", [128, 144], "bfloat16"), "ZS": ("sbuf", [128, 144], "bfloat16"),
-    "GW": ("sbuf", [128, 128], "bfloat16"), "BO": ("sbuf", [128, 128], "bfloat16"),
-    "PM": ("sbuf", [128, Q], "bfloat16"), "PM1": ("sbuf", [128, Q], "bfloat16"),
-    "S00": ("sbuf", [128, 128], "float32"), "S01": ("sbuf", [128, 128], "float32"), "S10": ("sbuf", [128, 128], "float32"), "S11": ("sbuf", [128, 128], "float32"),
-    "CM1": ("sbuf", [128, 384], "float32"),
-    "pI": ("sbuf", [128, Q], "int32"), "qI": ("sbuf", [128, Q], "int32"), "gI": ("sbuf", [128, Q], "int32"),
-    "nI": ("sbuf", [128, 144], "int32"), "mpI": ("sbuf", [128, 128], "int32"), "tI": ("sbuf", [128, Q], "int32"), "tI2": ("sbuf", [128, Q], "int32"), "c16I": ("sbuf", [128, Q], "int32"),
-    "b4": ("sbuf", [128, 8], "int32"), "b0F": ("sbuf", [128, 8], "float32"), "b1F": ("sbuf", [128, 8], "float32"),
-    "cF": ("sbuf", [128, 48], "float32"), "c256": ("sbuf", [128, 12], "int32"),
-    "X0": ("sbuf", [128, 384], "float32"), "X1": ("sbuf", [128, 384], "float32"),
-    "T0": ("sbuf", [128, 416], "float32"), "T1": ("sbuf", [128, 416], "float32"), "E0": ("sbuf", [128, 384], "float32"),
-    "tA": ("sbuf", [128, Q], "float32"), "tB": ("sbuf", [128, Q], "float32"), "tC": ("sbuf", [128, Q], "float32"), "tD": ("sbuf", [128, Q], "float32"),
-    "oB": ("sbuf", [128, 384], "bfloat16"),
-    "y_": ("sbuf", [128, Q], "float32"), "KEYC": ("sbuf", [128, Q], "float32"), "SLT": ("sbuf", [128, Q], "float32"), "tS": ("sbuf", [128, Q], "int32"),
-    "mkL": ("sbuf", [128, Q], "float32"), "mk": ("sbuf", [128, Q], "float32"), "hot": ("sbuf", [128, Q], "float32"),
-    "RL": ("sbuf", [128, Q], "float32"), "RS": ("sbuf", [128, Q], "float32"), "RC": ("sbuf", [128, Q], "float32"),
-    "bL": ("sbuf", [128, Q], "float32"), "bR": ("sbuf", [128, Q], "float32"), "bN": ("sbuf", [128, Q], "float32"),
-    "dif": ("sbuf", [128, Q], "float32"), "sL": ("sbuf", [128, Q], "int32"), "sM": ("sbuf", [128, Q], "int32"), "sC": ("sbuf", [128, Q], "int32"),
-    "LI": ("sbuf", [128, 320], "int32"), "LF": ("sbuf", [128, 480], "float32"), "Bf": ("sbuf", [128, 12], "bfloat16"),
-    "LST": ("sbuf", [128, 24], "uint16"),
-    "md": ("sbuf", [128, Q], "bfloat16"), "nD": ("sbuf", [128, Q], "bfloat16"),
-    "XL": ("psum", [128, 512], "float32"), "XS": ("psum", [128, 512], "float32"), "XC": ("psum", [128, 512], "float32"),
-    "VP1": ("psum", [128, 512], "float32"), "VP2": ("psum", [128, 512], "float32"), "VT": ("psum", [128, 512], "float32"),
-    "MI": ("psum", [128, 512], "float32"), "SWP": ("psum", [128, 512], "float32"),
-}
-PART = {"cv": ("cF", 0, 12), "cp": ("cF", 12, 12), "cb": ("cF", 24, 24), "us": ("LF", 372, 12), "wI": ("LI", 252, 24)}
+F32, BF, I32, U16 = "float32", "bfloat16", "int32", "uint16"
+SCRATCH = {}
+for _n, _w, _d in (
+        ("P", PW, BF), ("D", NPOS + Q, BF), ("AB0", NPOS + Q, BF), ("AB1", NPOS + Q, BF), ("SG", NPOS, BF), ("IC", NPOS, BF),
+        ("YE", NPOS, BF), ("CR", NPOS, BF), ("YL", Q, U16),
+        ("inL", Q, I32), ("inC", Q, I32), ("inO", Q, BF), ("inB", Q, BF), ("inLim", 8, I32), ("limF", 8, F32),
+        ("MSK", Q, F32), ("RSTL", Q, F32), ("RSTC", Q, F32), ("KT", Q, BF), ("CL", Q, BF), ("CC", Q, BF), ("ONE", 128, BF),
+        ("Z1", 144, BF), ("ZL", 144, BF), ("ZC", 144, BF), ("ZS", 144, BF), ("GW", 128, BF), ("BO", 128, BF), ("EY", 128, BF), ("NE", 128, BF),
+        ("PM", Q, BF), ("S00", 128, F32), ("S01", 128, F32), ("S10", 128, F32), ("S11", 128, F32),
+        ("pI", Q, I32), ("qI", Q, I32), ("kI", Q, I32), ("nI", 144, I32), ("mpI", 128, I32), ("c16I", Q, I32),
+        ("k1", Q, I32), ("k2", Q, I32), ("k3", Q, F32), ("k4", Q, F32), ("k5", 128, I32), ("k6", 128, I32), ("k7", 128, I32), ("k8", 12, I32), ("k9", 144, I32), ("k10", 144, I32),
+        ("b4", 8, I32), ("bF", 8, F32), ("cF", 48, F32), ("c256", 12, I32),
+        ("X0", 384, F32), ("X1", 384, F32), ("M0", 384, F32), ("M1", 384, F32), ("T0", 448, F32), ("T1", 448, F32), ("E0", 384, F32), ("oB", 384, BF),
+        ("tA", Q, F32), ("tB", Q, F32), ("tC", Q, F32), ("tD", Q, F32), ("tE", Q, F32), ("tF", Q, I32),
+        ("y_", Q, F32), ("KEYC", Q, F32), ("SLT", Q, F32), ("tS", Q, I32), ("mkL", Q, F32), ("mk", Q, F32), ("hot", Q, F32),
+        ("RLS", 384, F32), ("RC", Q, F32), ("bL", Q, F32), ("bR", Q, F32), ("bN", Q, F32),
+        ("dif", Q, F32), ("sL", Q, I32), ("sM", Q, I32), ("sC", Q, I32), ("LI", 312, I32), ("LF", 480, F32), ("Bf", 12, BF), ("LST", 24, U16),
+        ("md", Q, BF), ("nD", Q, BF)):
+    SCRATCH[_n] = ("sbuf", [128, _w], _d)
+for _n in ("XL", "XS", "XC", "VP1", "VP2", "VT", "OB", "SWP"):
+    SCRATCH[_n] = ("psum", [128, 512], F32)
 for _t in range(TV):
-    SCRATCH["DL%d" % _t] = ("sbuf", [128, Q], "float32")
-    SCRATCH["oL%d" % _t] = ("sbuf", [128, Q], "uint16")
-    SCRATCH["oC%d" % _t] = ("sbuf", [128, Q], "uint16")
-    SCRATCH["oV%d" % _t] = ("sbuf", [128, 2 * Q], "int32")
+    SCRATCH["PM1_%d" % (_t % 2)] = ("sbuf", [128, Q], BF)
+    SCRATCH["DL%d" % (_t % 2)] = ("sbuf", [128, Q], F32)
+    SCRATCH["oL%d" % (_t % 2)] = ("sbuf", [128, Q], U16)
+    SCRATCH["oC%d" % (_t % 2)] = ("sbuf", [128, Q], U16)
+    SCRATCH["oV%d" % (_t % 2)] = ("sbuf", [128, 2 * Q], I32)
     if _t:
-        SCRATCH["aL%d" % _t] = ("sbuf", [128, Q], "uint16")
-        SCRATCH["aC%d" % _t] = ("sbuf", [128, Q], "uint16")
-        SCRATCH["aV%d" % _t] = ("sbuf", [128, 2 * Q], "int32")
-SEMAPHORES = ["sv", "ss", "st", "sg", "snt"] + ["d%d" % i for i in range(16)] + [k + "%d" % t for k in ("qL", "qC", "qV") for t in range(1, TV)]
+        SCRATCH["aL%d" % _t] = ("sbuf", [128, Q], U16)
+        SCRATCH["aC%d" % _t] = ("sbuf", [128, Q], U16)
+        SCRATCH["aV%d" % _t] = ("sbuf", [128, 2 * Q], I32)
+SEMAPHORES = ["sv", "ss", "st", "sg"] + [k + i for k in ("lL", "lC", "lV") for i in "01"] + ["d%d" % i for i in range(16)] + [k + "%d" % t for k in ("qL", "qC", "qV") for t in range(1, TV)]
+PART = {"cv": ("cF", 0, 12), "cp": ("cF", 12, 12), "cb": ("cF", 24, 24),
+        "u": ("XS", 192, 12), "w": ("XS", 208, 12), "lm": ("XS", 224, 192), "RL": ("RLS", 0, 192), "RS": ("RLS", 192, 192)}
+BONUS = 4.0
+CY, FX, WK = 0.00092, 0.03, 0.08
 
 
 def rank_program(g, core, T, topo):
@@ -71,9 +58,7 @@ def rank_program(g, core, T, topo):
     af = ActivationFunctionType
     queues = {"v": g.vector, "s": g.scalar, "t": g.tensor, "g": g, "y": g.sync}
     semof = {"v": "sv", "s": "ss", "t": "st", "g": "sg"}
-    count = {}
-    clock = {e: {} for e in queues}
-    wr, rd = {}, {}
+    ops, wr, rd = [], {}, {}
     psum = {k for k in SCRATCH if SCRATCH[k][0] == "psum"}
 
     def A(name, lo=0, hi=None, st=1):
@@ -81,74 +66,73 @@ def rank_program(g, core, T, topo):
             name, base, n = PART[name]
             lo, hi = base + lo, base + (n if hi is None else hi)
         hi = SCRATCH[name][1][1] if hi is None else hi
-        return (name, lo, hi, T[name][:, lo:hi] if st == 1 else T[name][:, lo:hi:st])
+        return (name, lo, hi, T[name][:, lo:hi] if st == 1 else T[name][:, lo:hi:st], len(range(lo, hi, st)))
 
-    def emit(e, fn, R, Wt, sem=None, inc=1):
-        need = []
-        for (nm, lo, hi, _) in R:
-            for (l, h, o) in wr.get(nm, []):
-                if (l < hi and lo < h) or (nm in psum and o["e"] != e):
+    def emit(e, fn, R, Wt, cost, sem=None, inc=1, lat=0.0, deps=()):
+        need = list(deps)
+        for x in R:
+            for (l, h, o) in wr.get(x[0], []):
+                if (l < x[2] and x[1] < h) or (x[0] in psum and o["e"] != e):
                     need.append(o)
-            if nm in psum:
-                need += [o for (l, h, o) in rd.get(nm, []) if o["e"] != e]
-        for (nm, lo, hi, _) in Wt:
-            for (l, h, o) in wr.get(nm, []):
-                if (l < hi and lo < h) or (nm in psum and o["e"] != e):
+            if x[0] in psum:
+                need += [o for (l, h, o) in rd.get(x[0], []) if o["e"] != e]
+        for x in Wt:
+            for (l, h, o) in wr.get(x[0], []) + rd.get(x[0], []):
+                if (l < x[2] and x[1] < h) or (x[0] in psum and o["e"] != e):
                     need.append(o)
-            for (l, h, o) in rd.get(nm, []):
-                if (l < hi and lo < h) or (nm in psum and o["e"] != e):
-                    need.append(o)
-        want = {}
-        for o in need:
-            if o["v"] > want.get(o["s"], (0, None))[0]:
-                want[o["s"]] = (o["v"], o)
-        ck = clock[e]
-        for s in sorted(want, key=lambda s: -len(want[s][1]["c"])):
-            v, o = want[s]
-            if ck.get(s, 0) >= v:
-                continue
-            queues[e].wait_ge(T.sem[s], v)
-            for k, x in o["c"].items():
-                ck[k] = max(ck.get(k, 0), x)
-            ck[s] = max(ck.get(s, 0), v)
-        ins = fn(queues[e])
-        s = sem or semof[e]
-        if inc:
-            ins.then_inc(T.sem[s], inc)
-            count[s] = count.get(s, 0) + inc
-        me = {"e": "dma" if inc == 16 else e, "s": s, "v": count.get(s, 0), "c": dict(ck)}
-        for (nm, lo, hi, _) in R:
-            rd.setdefault(nm, []).append((lo, hi, me))
-        for (nm, lo, hi, a) in Wt:
-            wr[nm] = [x for x in wr.get(nm, []) if not (lo <= x[0] and x[1] <= hi)] + [(lo, hi, me)]
-            rd[nm] = [x for x in rd.get(nm, []) if not (lo <= x[0] and x[1] <= hi) or x[2] is me]
+        me = {"e": e, "fn": fn, "need": need, "cost": cost, "sem": sem or semof.get(e), "inc": inc, "lat": lat, "i": len(ops), "soft": [], "bonus": 0.0}
+        ops.append(me)
+        for x in R:
+            rd.setdefault(x[0], []).append((x[1], x[2], me))
+        for x in Wt:
+            nm, lo, hi = x[:3]
+            wr[nm] = [y for y in wr.get(nm, []) if not (lo <= y[0] and y[1] <= hi)] + [(lo, hi, me)]
+            rd[nm] = [y for y in rd.get(nm, []) if not (lo <= y[0] and y[1] <= hi) or y[2] is me]
         return me
+
+    def two(x):
+        return SCRATCH[x[0]][2] in (BF, U16)
+
+    def vc(o, ins):
+        n = max([x[4] for x in [o] + ins])
+        return FX + CY * max(64, n * (0.5 if all(two(x) for x in [o] + ins) else 1))
 
     def ts(o, i, s1, op0, s2=None, op1=None):
         if op1 is None:
-            emit("v", lambda q: q.tensor_scalar(o[3], i[3], s1, None, op0), [i], [o])
-        else:
-            sc = s2[3] if isinstance(s2, tuple) else s2
-            emit("v", lambda q: q.tensor_scalar(o[3], i[3], s1, sc, op0, op1), [i] + ([s2] if isinstance(s2, tuple) else []), [o])
+            return emit("v", lambda q: q.tensor_scalar(o[3], i[3], s1, None, op0), [i], [o], vc(o, [i]))
+        sc = s2[3] if isinstance(s2, tuple) else s2
+        return emit("v", lambda q: q.tensor_scalar(o[3], i[3], s1, sc, op0, op1), [i] + ([s2] if isinstance(s2, tuple) else []), [o], vc(o, [i]))
 
     def tt(o, a, b, o_):
-        emit("v", lambda q: q.tensor_tensor(o[3], a[3], b[3], o_), [a, b], [o])
+        k = 1 if a[0] in psum or b[0] in psum else 2
+        return emit("v", lambda q: q.tensor_tensor(o[3], a[3], b[3], o_), [a, b], [o], FX + CY * max(64, k * o[4]))
 
     def cp(o, i):
-        emit("v", lambda q: q.tensor_copy(o[3], i[3]), [i], [o])
+        return emit("v", lambda q: q.tensor_copy(o[3], i[3]), [i], [o], vc(o, [i]))
 
     def fill(o, c):
-        emit("v", lambda q: q.memset(o[3], c), [], [o])
+        return emit("v", lambda q: q.memset(o[3], c), [], [o], vc(o, []))
 
     def scan(o, d0, d1, init, p0, p1):
-        emit("v", lambda q: q.tensor_tensor_scan(o[3], d0[3], d1[3], init, p0, p1), [d0, d1], [o])
+        return emit("v", lambda q: q.tensor_tensor_scan(o[3], d0[3], d1[3], init, p0, p1), [d0, d1], [o], vc(o, [d0, d1]))
+
+    def vtr(o, i):
+        return emit("v", lambda q: q.transpose(o[3], i[3]), [i], [o], vc(o, [i]))
 
     def act(o, i, f, bias=0.0, scale=1.0, off=None):
         src = i[3].indirect(off[3]) if off else i[3]
-        emit("s", lambda q: q.activation(o[3], src, f, bias=bias, scale=scale), [i] + ([off] if off else []), [o])
+        f = af.Identity if f == af.Copy and bias else f
+        sc, extra = (scale[3], [scale]) if isinstance(scale, tuple) else (scale, [])
+        return emit("s", lambda q: q.activation(o[3], src, f, bias=bias, scale=sc), [i] + ([off] if off else []) + extra, [o],
+                    (0.065 + 1.56 * CY * o[4]) if off else FX + CY * max(64, o[4]))
+
+    def pool(o, fn):
+        return emit("g", fn, [], [o], 0.13 + 2 * CY * o[4])
 
     def iota(o, pattern, base, cm):
-        emit("g", lambda q: q.iota(o[3], pattern, base, cm), [], [o])
+        if SCRATCH[o[0]][2] == I32:
+            return pool(o, lambda q: q.iota(o[3], pattern, base, cm))
+        return pool(o, lambda q: q.iota(o[3], pattern, base, cm, allow_small_or_imprecise_dtypes=True))
 
     def mms(o, terms):
         R = [x for t in terms for x in t]
@@ -157,315 +141,390 @@ def rank_program(g, core, T, topo):
             for j, (l, r) in enumerate(terms):
                 ins = q.matmul(o[3], l[3], r[3], j == 0, j == len(terms) - 1)
             return ins
-        emit("t", go, R, [o])
+        k = 4 if SCRATCH[terms[0][0][0]][2] == F32 else 1
+        return emit("t", go, R, [o], FX + 0.00078 * k * max(64, o[4]) * len(terms))
 
     nd = [0]
 
-    def dma(e, o, i, R=[], Wt=[]):
-        emit(e, lambda q: q.dma_start(o, i), R, Wt, sem="d%d" % nd[0], inc=16)
+    def dma(e, o, i, R, Wt, lat):
+        s = "d%d" % nd[0]
         nd[0] += 1
+        return emit(e, lambda q: q.dma_start(o, i), R, Wt, 0.05, sem=s, inc=16, lat=lat)
 
-    def load(e, o, src):
-        dma(e, o[3], src, [], [o])
+    def LI(j, n=1):
+        return A("LI", 12 * j, 12 * (j + n))
 
-    def LI(j):
-        return A("LI", 12 * j, 12 * j + 12)
+    def LF(j, n=1):
+        return A("LF", 12 * j, 12 * (j + n))
 
-    def LF(j):
-        return A("LF", 12 * j, 12 * j + 12)
+    def send(k, nxt):
+        o, i = "a%s%d" % (k, nxt), "o%s%d" % (k, nxt % 2)
+        sl = "l%s%d" % (k, nxt % 2)
+        wid = SCRATCH[o][1][1]
+        lat = 1.6 + 128 * wid * (2 if k != "V" else 4) / 60e3
+        me = emit("g", lambda q: q.remote_dma(out_ap=T[o][:, :], in_ap=T[i][:, :], remote_sem=T.sem["q%s%d" % (k, nxt)], local_sem=T.sem[sl],
+                                              pid=pid, routing_id=rid, dma_engine_mask=emask), [A(i)], [], 0.6, sem=sl, inc=-neng, lat=lat)
+        net = {"e": "net", "need": [me], "cost": lat, "sem": "q%s%d" % (k, nxt), "v": neng, "inc": 0, "lat": 0.0, "i": len(ops), "soft": [], "bonus": 0.0}
+        ops.append(net)
+        wr[o] = [(0, wid, net)]
 
-    load("y", A("inL"), T.lem[:, :])
-    load("s", A("inC"), T.con[:, :])
-    load("y", A("inO"), T.org[:, :])
-    load("s", A("inB"), T.cnt[:, :])
-    load("y", A("inLim", 0, TV), T.lim[:, :])
-    load("s", A("AB0", NPOS, NPOS + Q), T.ex[:, :])
-    load("y", A("P", 0, W), T.prop[:, :])
+    dma("y", T.inC[:, :], T.con[:, :], [], [A("inC")], 2.0)
+    dma("y", T.inO[:, :], T.org[:, :], [], [A("inO")], 2.0)
+    dma("s", T.inB[:, :], T.cnt[:, :], [], [A("inB")], 2.0)
+    dma("y", T.inL[:, :], T.lem[:, :], [], [A("inL")], 2.2)
+    dma("s", T.AB0[:, NPOS:NPOS + Q], T.ex[:, :], [], [A("AB0", NPOS, NPOS + Q)], 2.2)
+    dma("y", T.inLim[:, 0:TV], T.lim[:, :], [], [A("inLim", 0, TV)], 2.2)
+    dma("y", T.P[:, 0:W], T.prop[:, :], [], [A("P", 0, W)], 6.0)
 
-    iota(A("pI"), [[0, Q]], 0, 1)
     iota(A("mpI"), [[1, 128]], 0, -1)
-    iota(A("gI"), [[0, 12], [1, 16]], 0, 0)
+    iota(A("pI"), [[0, Q]], 0, 1)
+    iota(A("kI"), [[0, 12], [1, 16]], 0, 0)
     iota(A("nI"), [[1, 144]], 0, 0)
     iota(A("c16I"), [[16, 12], [0, 16]], 0, 0)
-    emit("g", lambda q: q.iota(T.CM1[:, :], [[0, 12], [1, 2], [0, 16]], 0, 0, allow_small_or_imprecise_dtypes=True), [], [A("CM1")])
     iota(A("c256"), [[256, 12]], 0, 0)
-    kI = A("gI")
-    fill(A("T0", 0, 16), 0.0); fill(A("T0", 400, 416), 0.0); fill(A("T1", 0, 16), 0.0); fill(A("T1", 400, 416), 0.0)
+    iota(A("KT"), [[0, 12], [-1, 16]], 15, 0)
+    for x in ("T0", "T1"):
+        iota(A(x, 0, 32), [[0, 32]], 0, 0)
+        iota(A(x, 416, 448), [[0, 32]], 0, 0)
+    iota(A("P", W, PW), [[0, PW - W]], 0, 0)
+    iota(A("D", NPOS, NPOS + Q), [[0, Q]], 0, 0)
+    for x in ("bL", "bR", "bN"):
+        iota(A(x), [[0, Q]], 0, 0)
+    kI = A("kI")
+    b0, b1 = A("bF", 0, 1), A("bF", 1, 2)
     ts(A("b4", 0, 1), A("pI", 0, 1), 16, op.bitwise_and)
-    ts(A("b0F", 0, 1), A("b4", 0, 1), 0, op.is_equal)
-    ts(A("b1F", 0, 1), A("b4", 0, 1), 16, op.is_equal)
-    ts(A("S00"), A("mpI"), 0, op.is_equal, A("b0F", 0, 1), op.mult)
-    ts(A("S11"), A("mpI"), 0, op.is_equal, A("b1F", 0, 1), op.mult)
-    ts(A("S01"), A("mpI"), 16, op.is_equal, A("b0F", 0, 1), op.mult)
-    ts(A("S10"), A("mpI"), -16, op.is_equal, A("b1F", 0, 1), op.mult)
+    ts(b0, A("b4", 0, 1), 0, op.is_equal)
+    ts(b1, A("b4", 0, 1), 16, op.is_equal)
+    ts(A("S00"), A("mpI"), 0, op.is_equal, b0, op.mult)
+    ts(A("S11"), A("mpI"), 0, op.is_equal, b1, op.mult)
+    ts(A("S01"), A("mpI"), 16, op.is_equal, b0, op.mult)
+    ts(A("S10"), A("mpI"), -16, op.is_equal, b1, op.mult)
 
-    def swap(x):
-        tt(A("T1", 16, 400), x, A("CM1"), op.mult)
-        tt(A("T0", 16, 400), x, A("T1", 16, 400), op.subtract)
-        mms(A("SWP", 0, 384), [(A("S00"), A("T0", 16, 400)), (A("S11"), A("T1", 16, 400)), (A("S01"), A("T1", 32, 416)), (A("S10"), A("T0", 0, 384))])
+    def turn(x):
+        act(A("M0"), x, af.Copy, scale=b0)
+        act(A("M1"), x, af.Copy, scale=b1)
+        vtr(A("T0", 32, 416), A("M0"))
+        vtr(A("T1", 32, 416), A("M1"))
+        mms(A("SWP", 0, 384), [(A("S00"), A("T0", 32, 416)), (A("S11"), A("T1", 32, 416)), (A("S01"), A("T1", 48, 432)), (A("S10"), A("T0", 16, 400))])
 
-    def vtr(o, i):
-        emit("v", lambda q: q.transpose(o[3], i[3]), [i], [o])
+    act(A("XL", 0, Q), A("inO"), af.Copy, scale=-16384.0, bias=15 * 16384.0)
+    act(A("XC", 0, Q), A("inB"), af.Copy, scale=262144.0)
+    act(A("OB", 0, Q), A("inB"), af.Copy, scale=2.0 - 262144.0, bias=2105344.0)
     cp(A("X0", 0, Q), A("inL"))
-    ts(A("tA"), A("inO"), -16384, op.mult, 15 * 16384, op.add)
     ts(A("tB"), A("inC"), 0, op.max, 2, op.mult)
-    tt(A("tA"), A("tA"), A("tB"), op.add)
-    ts(A("tB"), A("inB"), 1 << 18, op.mult)
-    tt(A("tA"), A("tA"), A("tB"), op.add)
-    ts(A("tC"), A("inB"), 2 - (1 << 18), op.mult, (1 << 21) + (1 << 13), op.add)
     ts(A("tD"), A("inC"), 0, op.is_lt)
-    tt(A("tC"), A("tC"), A("tD"), op.mult)
-    tt(A("X0", Q, 2 * Q), A("tA"), A("tC"), op.add)
-    vtr(A("X1"), A("X0"))
-    swap(A("X1"))
+    tt(A("tA"), A("XL", 0, Q), A("tB"), op.add)
+    tt(A("tC"), A("XC", 0, Q), A("tA"), op.add)
+    tt(A("tE"), A("OB", 0, Q), A("tD"), op.mult)
+    tt(A("X0", Q, 2 * Q), A("tC"), A("tE"), op.add)
+    turn(A("X0"))
     K13, K21 = A("VP1", 0, Q), A("VP1", Q, 2 * Q)
     KC, TH = A("VP2", 0, Q), A("VP2", Q, 2 * Q)
     TA, TB = A("VT", 0, Q), A("VT", Q, 2 * Q)
     ts(K13, kI, -8192, op.mult, 4096 + 15 * 8192, op.add)
     cp(A("oL0"), A("SWP", 0, Q))
+    act(A("X1", 0, Q), A("SWP", 0, Q), af.Copy)
     cp(A("oV0", Q, 2 * Q), A("SWP", Q, 2 * Q))
-    cp(A("tA"), A("SWP", 0, Q))
-    tt(A("oV0", 0, Q), A("tA"), K13, op.add)
+    tt(A("oV0", 0, Q), A("X1", 0, Q), K13, op.add)
 
     def coff(t):
-        ts(A("sC"), A("oV%d" % t, Q, 2 * Q), 1, op.arith_shift_right, 8191, op.bitwise_and)
-        cp(A("oC%d" % t), A("sC"))
+        ts(A("sC"), A("oV%d" % (t % 2), Q, 2 * Q), 1, op.arith_shift_right, 8191, op.bitwise_and)
+        cp(A("oC%d" % (t % 2)), A("sC"))
     coff(0)
     ts(A("qI"), A("pI"), 15, op.bitwise_and)
-    tt(A("tI"), A("c16I"), A("qI"), op.add)
-    cp(A("YL"), A("tI"))
-    fill(A("P", W, PW), 0.0)
-    fill(A("D", NPOS, NPOS + Q), 0.0)
+    tt(A("k1"), A("c16I"), A("qI"), op.add)
+    cp(A("YL"), A("k1"))
+
+    def chain(seq):
+        for x, y in zip(seq, seq[1:]):
+            y["soft"].append(x)
 
     def yexp(p):
-        n = Q // CH
-        for c in range(CH):
-            act(A("YE", c * NPOS // CH, (c + 1) * NPOS // CH), A("AB%d" % p, NPOS, NPOS + Q), af.Copy, off=A("YL", c * n, (c + 1) * n))
+        seq = [act(A("YE", 16 * a, 16 * b), A("AB%d" % p, NPOS, NPOS + Q), af.Copy, off=A("YL", a, b)) for a, b in LCH]
+        chain(seq)
+        seq[0]["bonus"] = BONUS
     yexp(0)
-    ts(A("tI", 0, 144), A("pI", 0, 144), 240, op.bitwise_and)
-    tt(A("tI2", 0, 144), A("nI"), A("tI", 0, 144), op.subtract)
-    for z, s in (("ZL", 2.0 ** 25), ("ZS", -16.0), ("ZC", 2.0 ** 26), ("Z1", 1.0)):
-        ts(A(z), A("tI2", 0, 144), 15, op.is_equal, s, op.mult)
+    ts(A("k9"), A("pI", 0, 144), 240, op.bitwise_and)
+    tt(A("k10"), A("nI"), A("k9"), op.subtract)
+    ts(A("Z1"), A("k10"), 15, op.is_equal)
+    for z, s in (("ZL", 2.0 ** 25), ("ZS", -16.0), ("ZC", 2.0 ** 26)):
+        act(A(z), A("Z1"), af.Copy, scale=s)
+    ts(A("EY"), A("mpI"), 0, op.is_equal)
+    act(A("NE"), A("EY"), af.Copy, scale=-1.0)
     fill(A("ONE"), 1.0 / 128)
     fill(A("CL"), 2.0 ** 25)
     fill(A("CC"), -7.5 * 2.0 ** 26)
-    ts(A("KT"), kI, -1, op.mult, 15, op.add)
     ts(A("MSK"), kI, 0, op.is_gt)
-
-    def gather_l(t):
-        n = Q // CH
-        lst = ("aL%d" if t else "oL%d") % t
-        for c in range(CH):
-            lo, hi = c * NPOS // CH, (c + 1) * NPOS // CH
-            off, ye, o = A(lst, c * n, (c + 1) * n), A("YE", lo, hi), A("D", lo, hi)
-            emit("v", lambda q: q.tensor_tensor(o[3], T.P[:, :].indirect(off[3]), ye[3], op.subtract), [A("P"), off, ye], [o])
-            act(A("SG", lo, hi), o, af.Sign, bias=-0.5)
-            act(A("AB%d" % (t % 2), lo, hi), o, af.Abs)
-            cnt("XL", "SG", "ZL", "CL", c)
-            cnt("XS", "AB%d" % (t % 2), "ZS", "KT", c)
-
-    def gather_c(t):
-        n = Q // CH
-        lst = ("aC%d" if t else "oC%d") % t
-        for c in range(CH):
-            lo, hi = c * NPOS // CH, (c + 1) * NPOS // CH
-            off, ye, o = A(lst, c * n, (c + 1) * n), A("YE", lo, hi), A("IC", lo, hi)
-            emit("v", lambda q: q.tensor_tensor(o[3], T.P[:, :].indirect(off[3]), ye[3], op.is_gt), [A("P"), off, ye], [o])
-            cnt("XC", "IC", "ZC", "CC", c)
-
-    def cnt(x, src, z, const, c):
-        n = Q // CH
-        mms(A(x, c * n, (c + 1) * n), [(A("ONE"), A(const, c * n, (c + 1) * n))] +
-            [(A(z, 15 - q, 143 - q), A(src, c * n * 16 + q, (c + 1) * n * 16, 16)) for q in range(16)])
-
-    def usum(p):
-        mms(A("MI", 0, 12), [(A("Z1", 15 - q, 143 - q), A("AB%d" % p, NPOS + q, NPOS + Q, 16)) for q in range(16)])
-        act(A("us"), A("MI", 0, 12), af.Copy)
-
-    gather_l(0)
     ts(K21, kI, -(1 << 21), op.mult, 15 * (1 << 21) - (1 << 24) + (1 << 13), op.add)
     ts(KC, kI, -2, op.mult, 30 - (1 << 24) - (1 << 13), op.add)
-    ts(A("RSTL"), A("MSK"), 2.0 ** 27, op.mult, -2.0 ** 20, op.add)
-    ts(A("RSTC"), A("MSK"), 2.0 ** 28, op.mult, -2.0 ** 27, op.add)
+    act(A("RSTL"), A("MSK"), af.Copy, scale=2.0 ** 27, bias=-2.0 ** 20)
+    act(A("RSTC"), A("MSK"), af.Copy, scale=2.0 ** 28, bias=-2.0 ** 27)
     cp(A("limF", 0, TV), A("inLim", 0, TV))
-    tt(A("tI"), kI, A("qI"), op.subtract)
-    ts(A("tA"), A("tI"), 0, op.is_equal)
-    ts(A("tB"), A("tI"), 1, op.is_equal)
-    tt(A("PM"), A("tA"), A("tB"), op.subtract)
-    ts(A("tI2", 0, 128), A("nI", 0, 128), 240, op.bitwise_and)
-    ts(A("tI", 0, 128), A("pI", 0, 128), 240, op.bitwise_and)
-    tt(A("BO"), A("tI2", 0, 128), A("tI", 0, 128), op.is_equal)
-    ts(A("tI", 0, 128), A("mpI"), 15, op.bitwise_and)
-    ts(A("GW"), A("tI", 0, 128), 0, op.is_equal)
-    tt(A("tI", 0, 12), A("c16I", 0, Q, 16), A("qI", 0, 12), op.add)
-    cp(A("cv"), A("tI", 0, 12))
-    ts(A("cb", 0, 12), A("cv"), NPOS, op.add)
-    ts(A("cb", 12, 24), A("cv"), DUMP, op.add)
-    tt(A("cp"), A("c256"), A("qI", 0, 12), op.add)
-    ts(A("cp"), A("cp"), 240, op.add)
-    tt(A("cp"), A("cp"), A("cb", 0, 12), op.subtract)
-    fill(A("bL"), 0.0); fill(A("bR"), 0.0); fill(A("bN"), 0.0)
-    usum(0)
+    tt(A("k2"), kI, A("qI"), op.subtract)
+    ts(A("k3"), A("k2"), 0, op.is_equal)
+    ts(A("k4"), A("k2"), 1, op.is_equal)
+    tt(A("PM"), A("k3"), A("k4"), op.subtract)
+    ts(A("k5"), A("nI", 0, 128), 240, op.bitwise_and)
+    ts(A("k6"), A("pI", 0, 128), 240, op.bitwise_and)
+    tt(A("BO"), A("k5"), A("k6"), op.is_equal)
+    ts(A("k7"), A("mpI"), 15, op.bitwise_and)
+    ts(A("GW"), A("k7"), 0, op.is_equal, 2.0 ** 18, op.mult)
+    tt(A("k8"), A("c16I", 0, Q, 16), A("qI", 0, 12), op.add)
+    cp(A("cv"), A("k8"))
+    ts(A("cb", 0, 12), A("k8"), NPOS, op.add)
+    ts(A("cb", 12, 24), A("k8"), DUMP, op.add)
+    tt(A("tA", 0, 12), A("c256"), A("qI", 0, 12), op.add)
+    ts(A("tB", 0, 12), A("tA", 0, 12), 240, op.add)
+    tt(A("cp"), A("tB", 0, 12), A("cb", 0, 12), op.subtract)
+
+    def cnt(x, src, z, const, a, b):
+        mms(A(x, a, b), [(A("ONE"), A(const, a, b))] + [(A(z, 15 - q, 143 - q), A(src, a * 16 + q, b * 16, 16)) for q in range(16)])
+
+    def gather_l(t):
+        lst, ab = ("aL%d" if t else "oL%d") % t, "AB%d" % (t % 2)
+
+        def one(a, b):
+            off, ye, o = A(lst, a, b), A("YE", 16 * a, 16 * b), A("D", 16 * a, 16 * b)
+            me = emit("v", lambda q: q.tensor_tensor(o[3], T.P[:, :].indirect(off[3]), ye[3], op.subtract), [A("P"), off, ye], [o], 0.05 + 1.56 * CY * o[4])
+            act(A("SG", 16 * a, 16 * b), o, af.Sign, bias=-0.5)
+            act(A(ab, 16 * a, 16 * b), o, af.Abs)
+            cnt("XL", "SG", "ZL", "CL", a, b)
+            cnt("XS", ab, "ZS", "KT", a, b)
+            return me
+        return [one(a, b) for a, b in LCH]
+
+    def gather_c(t):
+        lst = ("aC%d" if t else "oC%d") % t
+
+        def one(a, b):
+            off, ye, o = A(lst, a, b), A("YE", 16 * a, 16 * b), A("IC", 16 * a, 16 * b)
+            me = emit("v", lambda q: q.tensor_tensor(o[3], T.P[:, :].indirect(off[3]), ye[3], op.is_gt), [A("P"), off, ye], [o], 0.05 + 1.56 * CY * o[4])
+            cnt("XC", "IC", "ZC", "CC", a, b)
+            return me
+        return [one(a, b) for a, b in CCH]
+
+    def gather_s(t):
+        lst = ("aC%d" if t else "oC%d") % t
+        for a, b in SCH:
+            act(A("CR", 16 * a, 16 * b), A("P"), af.Copy, off=A(lst, a, b))
+        for j, (a, b) in enumerate(SCH):
+            ps = A(("OB", "SWP")[j % 2], 0, 16 * (b - a))
+            mms(ps, [(A("EY"), A("CR", 16 * a, 16 * b)), (A("NE"), A("YE", 16 * a, 16 * b))])
+            act(A("IC", 16 * a, 16 * b), ps, af.Sign, bias=-0.5)
+        if SCH:
+            cnt("XC", "IC", "ZL", "CL", SCH[0][0], SCH[-1][1])
+
+    def usum(p):
+        mms(A("u"), [(A("Z1", 15 - q, 143 - q), A("AB%d" % p, NPOS + q, NPOS + Q, 16)) for q in range(16)])
+        act(LF(36), A("u"), af.Copy)
+        act(LF(37), A("u"), af.Copy)
+        return cp(LI(2), LF(36))
+
+    def wcount(t):
+        d = "DL%d" % (t % 2)
+        return [cp(LI(21), A("w")), ts(LI(22), LI(21), 3 << 18, op.bitwise_and), tt(starts(d, 0), starts(d, 0), LI(22), op.add),
+                scan(TH, A("MSK"), A(d), 0.0, op.mult, op.add)]
 
     def lims(t):
-        ts(A("PM1"), A("PM"), A("limF", t, t + 1)[3], op.mult)
-        mms(A("SWP", 0, Q), [(A("BO"), A("PM1"))])
-        act(A("DL%d" % t), A("SWP", 0, Q), af.Copy, scale=2.0 ** 18)
+        act(A("PM1_%d" % (t % 2)), A("PM"), af.Copy, scale=A("limF", t, t + 1))
+        mms(A("lm"), [(A("BO"), A("PM1_%d" % (t % 2)))])
+        act(A("DL%d" % (t % 2)), A("lm"), af.Copy, scale=2.0 ** 18)
+
+    def pnew(to, y):
+        return emit("v", lambda q: q.tensor_tensor(T.P[:, :].indirect(to[3]), T.md[:, :], y[3], op.add), [A("md"), y, to], [A("P")], 0.05 + 3.8 * CY * Q)
 
     def starts(name, a=15):
-        return A(name, a, Q, 16)
+        return A(name, a, None, 16) if name not in PART else A(name, a, PART[name][2], 16)
 
+    lims(0)
     for t in range(TV):
         p = t % 2
         AB, yv = A("AB%d" % p), A("AB%d" % p, NPOS, NPOS + Q)
-        if t:
-            gather_l(t)
+        nxt = t + 1
+        last = nxt == TV
         pv = ("aV%d" if t else "oV%d") % t
         Lp, V = A(pv, 0, Q), A(pv, Q, 2 * Q)
-        if t == 0:
-            lims(0)
-            scan(TH, A("MSK"), A("DL0"), 0.0, op.mult, op.add)
-        gather_c(t)
+        seq = gather_l(t)
+        wseq = wcount(t) if t else [scan(TH, A("MSK"), A("DL0"), 0.0, op.mult, op.add)]
+        seq += gather_c(t)
+        seq.append(usum(p))
+        wseq[0]["soft"].append(seq[0])
+        chain(seq)
+        gather_s(t)
         tt(TA, V, TH, op.is_ge)
         tt(A("y_"), TA, V, op.add)
         ts(A("tS"), V, 15 << 18, op.bitwise_and, 9, op.arith_shift_right)
         tt(A("KEYC"), A("y_"), K21, op.add)
         tt(A("SLT"), A("tS"), KC, op.add)
+        if not last:
+            lims(nxt)
         tt(A("mkL"), A("XL", 0, Q), Lp, op.min)
         scan(A("RS"), A("RSTL"), A("XS", 0, Q), -2.0 ** 20, op.min, op.max)
         scan(A("RL"), A("RSTL"), A("mkL"), -2.0 ** 20, op.min, op.max)
-        RL, RS, RC = starts("RL"), starts("RS"), starts("RC")
-        cp(LI(0), RL)
-        cp(LI(1), RS)
-        tt(LI(10), A("us"), A("us"), op.mult)
-        ts(LI(2), LI(0), 4095, op.bitwise_and)
-        ts(LI(11), LI(10), 5, op.arith_shift_right)
-        tt(LI(3), LI(2), A("us"), op.mult)
-        ts(LF(0), A("us"), 37, op.mult, t, op.add)
-        ts(LI(4), LI(3), 5, op.arith_shift_right)
-        tt(LI(12), LI(11), LF(0), op.add)
-        tt(LI(5), LI(4), LI(2), op.add)
-        ts(LI(13), LI(12), 4095, op.bitwise_and)
-        if t:
-            ts(LI(6), LI(5), 97 * t, op.add)
-        ts(LI(14), LI(1), 15, op.bitwise_and)
-        ts(LI(7), LI(6 if t else 5), 3840, op.bitwise_and)
-        ts(LF(1), LI(14), 8192, op.mult, 4096, op.add)
-        tt(LF(2), A("cv"), LI(2), op.subtract)
-        tt(LF(3), LF(1), LI(13), op.add)
-        tt(LF(4), LI(7), LF(2), op.add)
-        ts(LF(5), RL, 0, op.is_lt)
-        tt(LF(6), LF(4), RL, op.add)
-        tt(LF(7), LF(5), LF(3), op.mult)
+        RL, RC = starts("RL"), starts("RC")
+        act(LF(0), LF(36), af.Copy, scale=37.0, bias=float(t))
+        act(LF(1), RL, af.Copy, bias=97.0 * t)
+        act(LF(10), RL, af.Copy, scale=2.0, bias=-8192.0)
+        cp(LI(0, 2), A("RLS", 15, 384, 16))
+        ts(LI(3), LI(0), 4095, op.bitwise_and)
+        tt(LI(4, 2), LI(2, 2), LF(36, 2), op.mult)
+        ts(LI(6, 2), LI(4, 2), 5, op.arith_shift_right)
+        tt(LI(8, 2), LI(6, 2), LF(0, 2), op.add)
+        ts(LI(10), LI(8), 4095, op.bitwise_and)
+        ts(LI(11), LI(9), 3840, op.bitwise_and)
+        ts(LI(12), LI(1), 15, op.bitwise_and)
+        ts(LF(2), LI(12), 8192, op.mult, 4096, op.add)
+        tt(LF(3), LF(2), LI(10), op.add)
+        tt(LF(4), A("cv"), LI(3), op.subtract)
+        tt(LF(5), LI(11), LF(4), op.add)
+        tt(LF(6), LF(5), RL, op.add)
+        ts(LF(7), RL, 0, op.is_lt)
         ts(LF(8), RL, 0, op.is_ge)
-        tt(LF(9), LF(6), LF(7), op.max)
-        ts(LI(15), LI(0), 9, op.arith_shift_right, 240, op.bitwise_and)
-        ts(LF(10), RL, 2, op.mult, -8192, op.add)
-        tt(LF(11), A("cp"), LI(15), op.subtract)
-        ts(LF(12), LI(7), -DUMP, op.add)
+        tt(LF(9), LF(7), LF(3), op.mult)
+        tt(LF(11), LF(6), LF(9), op.max)
+        ts(LI(13), LI(0), 9, op.arith_shift_right, 240, op.bitwise_and)
+        tt(LF(12), A("cp"), LI(13), op.subtract)
+        ts(LF(13), LI(11), -DUMP, op.add)
         tt(TA, A("XC", 0, Q), A("KEYC"), op.min)
         tt(A("mk"), TA, A("SLT"), op.max)
         scan(A("RC"), A("RSTC"), A("mk"), -2.0 ** 27, op.min, op.max)
         cp(LI(16), RC)
-        ts(LF(13), RC, -2.0 ** 24, op.is_lt)
+        ts(LF(14), RC, -2.0 ** 24, op.is_lt)
+        ts(LF(15), RC, -2.0 ** 24, op.is_ge)
         ts(LI(17), LI(16), 1, op.bitwise_and)
         ts(LI(18), LI(16), 0x3FFFE, op.bitwise_and, 1, op.arith_shift_right)
-        tt(LF(14), LF(13), LF(9), op.mult)
-        tt(LF(15), LI(17), LI(18), op.mult)
-        ts(LI(19), LI(16), 0x1FDFFE, op.bitwise_and)
-        ts(LI(20), LI(16), 0x3C000, op.bitwise_and)
-        tt(starts("bL", 0), LF(14), LF(15), op.add)
-        tt(LF(16), LF(13), LF(8), op.mult)
+        tt(LF(16), LF(14), LF(11), op.mult)
+        tt(LF(17), LI(17), LI(18), op.mult)
+        tt(starts("bL", 0), LF(16), LF(17), op.add)
         scan(TA, A("MSK"), A("bL"), 0.0, op.mult, op.add)
-        tt(LF(18), LF(11), LF(16), op.mult)
         tt(A("dif"), TA, Lp, op.subtract)
-        tt(LF(19), LF(12), LF(16), op.mult)
         ts(TB, A("dif"), -4096, op.max, 4096, op.min)
-        ts(LF(17), RC, -2.0 ** 24, op.is_ge)
         tt(A("sL"), TB, Lp, op.add)
-        tt(A("LF", 240, 264), A("LF", 216, 240), A("cb"), op.add)
         ts(A("sM"), A("sL"), 4095, op.bitwise_and)
-        cp(A("LST"), A("LF", 240, 264))
-        nxt = t + 1
-        last = nxt == TV
-
-        def send(nm, k):
-            o, i = T["a%s%d" % (k, nxt)], T["o%s%d" % (k, nxt)]
-            emit("g", lambda q: q.remote_dma(out_ap=o[:, :], in_ap=i[:, :], remote_sem=T.sem["q%s%d" % (k, nxt)], local_sem=T.sem.snt,
-                                             pid=pid, routing_id=rid, dma_engine_mask=emask), [A("o%s%d" % (k, nxt))], [], inc=0)
-            count["snt"] = count.get("snt", 0) + neng
-            nm_ = "a%s%d" % (k, nxt)
-            wr[nm_] = [(0, SCRATCH[nm_][1][1], {"e": "net", "s": "q%s%d" % (k, nxt), "v": neng, "c": {}})]
         if not last:
-            cp(A("oL%d" % nxt), A("sM"))
-            send("oL", "L")
+            cp(A("oL%d" % (nxt % 2)), A("sM"))
+            send("L", nxt)
+        tt(LF(18), LF(14), LF(8), op.mult)
+        tt(LF(20), LF(12), LF(18), op.mult)
+        tt(LF(21), LF(13), LF(18), op.mult)
+        tt(LF(22, 2), LF(20, 2), A("cb"), op.add)
+        cp(A("LST"), LF(22, 2))
         PL, NL = A("LST", 0, 12), A("LST", 12, 24)
+        act(A("AB%d" % (1 - p), NPOS, NPOS + Q), AB, af.Copy, off=PL)
         act(A("nD"), A("D"), af.Relu, scale=-1.0, off=PL)
         act(A("md"), A("nD"), af.Copy, scale=-1.0)
-        act(A("AB%d" % (1 - p), NPOS, NPOS + Q), AB, af.Copy, off=PL)
-        tt(LF(21), LF(17), LF(8), op.max)
-        ts(LF(22), LI(19), 1 << 18, op.add)
-        tt(starts("bR", 0), LF(21), RC, op.mult)
-        ts(LF(23), LI(20), (1 << 21) + (1 << 13), op.add)
+        tt(LF(24), LF(15), LF(8), op.max)
+        tt(starts("bR", 0), LF(24), RC, op.mult)
+        ts(LI(19), LI(16), 0x1FDFFE, op.bitwise_and)
+        ts(LI(20), LI(16), 0x3C000, op.bitwise_and)
+        ts(LF(25), LI(19), 1 << 18, op.add)
+        ts(LF(26), LI(20), (1 << 21) + (1 << 13), op.add)
+        tt(LF(27), LF(26), LI(17), op.mult)
+        tt(LF(28), LF(25), LF(27), op.max)
+        tt(LF(29), LF(10), LF(14), op.mult)
+        tt(LF(30), LF(28), LF(15), op.mult)
+        tt(starts("bN", 0), LF(29), LF(30), op.add)
         scan(TA, A("MSK"), A("bR"), 0.0, op.mult, op.add)
-        tt(LF(24), LF(23), LI(17), op.mult)
-        tt(LF(25), LF(22), LF(24), op.max)
-        tt(LF(26), LF(10), LF(13), op.mult)
         tt(A("hot"), A("mk"), TA, op.is_equal)
-        tt(LF(27), LF(25), LF(17), op.mult)
-        tt(starts("bN", 0), LF(26), LF(27), op.add)
-        scan(TA, A("MSK"), A("bN"), 0.0, op.mult, op.add)
-        tt(TB, TA, V, op.subtract)
-        ov = "oV%d" % nxt if not last else "oV0"
-        tt(TA, A("hot"), TB, op.mult)
-        pnew = lambda: emit("v", lambda q: q.tensor_tensor(T.P[:, :].indirect(NL[3]), T.md[:, :], yv[3], op.add), [A("md"), yv, NL], [A("P")])
-        if last:
-            pnew()
-            tt(A(ov, Q, 2 * Q), TA, V, op.add)
-            break
-        tt(A(ov, Q, 2 * Q), TA, V, op.add)
-        coff(nxt)
-        send("oC", "C")
-        tt(A(ov, 0, Q), A("sM"), K13, op.add)
-        send("oV", "V")
-        yexp(1 - p)
-        pnew()
-        cp(A("Bf"), LF(17))
-        mms(A("MI", 0, 12), [(A("GW"), A("Bf"))])
-        cp(A("wI", 0, 12), A("MI", 0, 12))
-        ts(A("wI", 12, 24), A("wI", 0, 12), 3, op.bitwise_and)
-        ts(LF(30), A("wI", 12, 24), 1 << 18, op.mult)
-        lims(nxt)
-        d = "DL%d" % nxt
-        tt(starts(d, 0), starts(d, 0), LF(30), op.add)
-        scan(TH, A("MSK"), A(d), 0.0, op.mult, op.add)
-        usum(1 - p)
+        scan(TB, A("MSK"), A("bN"), 0.0, op.mult, op.add)
+        tt(A("dif"), TB, V, op.subtract)
+        tt(TA, A("hot"), A("dif"), op.mult)
+        on = "oV%d" % (nxt % 2)
+        tt(A(on, Q, 2 * Q), TA, V, op.add)
 
-    dma("y", T.zp[:, :], T.P[:, 0:W], [A("P", 0, W)])
-    dma("y", T.zy[:, :], T.AB0[:, NPOS:NPOS + Q], [A("AB0", NPOS, NPOS + Q)])
-    VN = A("oV0", Q, 2 * Q)
+        pnew(NL, yv)["bonus"] = BONUS if last else 0.0
+        if last:
+            break
+        coff(nxt)
+        send("C", nxt)
+        tt(A(on, 0, Q), A("sM"), K13, op.add)
+        send("V", nxt)
+        yexp(1 - p)
+        cp(A("Bf"), LF(15))
+        mms(A("w"), [(A("GW"), A("Bf"))])
+
+    dma("y", T.zp[:, :], T.P[:, 0:W], [A("P", 0, W)], [], 6.0)
+    pe = TV % 2
+    dma("y", T.zy[:, :], T["AB%d" % pe][:, NPOS:NPOS + Q], [A("AB%d" % pe, NPOS, NPOS + Q)], [], 2.0)
+    VN = A("oV%d" % pe, Q, 2 * Q)
     cp(A("X0", 0, Q), A("sM"))
-    ts(A("sL"), VN, 1, op.arith_shift_right, 8191, op.bitwise_and)
-    ts(A("tA"), A("sL"), 4096, op.is_lt)
-    ts(A("tB"), A("sL"), 1, op.add)
-    ts(A("sM"), VN, 14, op.arith_shift_right, 15, op.bitwise_and)
-    tt(A("tC"), A("tA"), A("tB"), op.mult)
+    ts(A("tF"), VN, 1, op.arith_shift_right, 8191, op.bitwise_and)
+    ts(A("tA"), A("tF"), 4096, op.is_lt)
+    ts(TB, A("tF"), 1, op.add)
+    tt(A("tC"), A("tA"), TB, op.mult)
     ts(A("X0", Q, 2 * Q), A("tC"), -1, op.add)
-    ts(A("X1", 0, Q), A("sM"), -1, op.mult, 15, op.add)
+    turn(A("X0"))
+    ts(A("sL"), VN, 14, op.arith_shift_right, 15, op.bitwise_and)
+    ts(A("X1", 0, Q), A("sL"), -1, op.mult, 15, op.add)
     ts(A("sC"), VN, 18, op.arith_shift_right, 7, op.bitwise_and)
-    ts(A("tB"), A("sL"), -4096, op.add, 0, op.max)
-    tt(A("X1", Q, 2 * Q), A("sC"), A("tB"), op.add)
-    swap(A("X0"))
-    cp(A("E0"), A("SWP", 0, 384))
-    swap(A("X1"))
-    vtr(A("X0"), A("E0"))
-    dma("y", T.zl[:, :], T.X0[:, 0:Q], [A("X0", 0, Q)])
-    dma("s", T.zc[:, :], T.X0[:, Q:2 * Q], [A("X0", Q, 2 * Q)])
-    cp(A("E0"), A("SWP", 0, 384))
-    vtr(A("X1"), A("E0"))
-    cp(A("oB"), A("X1"))
-    dma("y", T.zo[:, :], T.oB[:, 0:Q], [A("oB", 0, Q)])
-    dma("s", T.zb[:, :], T.oB[:, Q:2 * Q], [A("oB", Q, 2 * Q)])
+    ts(TB, A("tF"), -4096, op.add, 0, op.max)
+    tt(A("X1", Q, 2 * Q), A("sC"), TB, op.add)
+    act(A("E0"), A("SWP", 0, 384), af.Copy)
+    dma("y", T.zl[:, :], T.E0[:, 0:Q], [A("E0", 0, Q)], [], 2.0)
+    dma("y", T.zc[:, :], T.E0[:, Q:2 * Q], [A("E0", Q, 2 * Q)], [], 2.0)
+    turn(A("X1"))
+    act(A("oB"), A("SWP", 0, 384), af.Copy)
+    dma("y", T.zo[:, :], T.oB[:, 0:Q], [A("oB", 0, Q)], [], 2.0)
+    dma("y", T.zb[:, :], T.oB[:, Q:2 * Q], [A("oB", Q, 2 * Q)], [], 2.0)
+
+    succ = [[] for _ in ops]
+    for o in ops:
+        o["need"] = list({x["i"]: x for x in o["need"]}.values())
+        o["all"] = list({x["i"]: x for x in o["need"] + o["soft"]}.values())
+        for x in o["all"]:
+            succ[x["i"]].append(o)
+    for o in reversed(ops):
+        o["pri"] = o["bonus"] + o["cost"] + o["lat"] + max([0.0] + [s["pri"] + WK for s in succ[o["i"]]])
+    left = {o["i"]: len(o["all"]) for o in ops}
+    free = {e: 0.0 for e in list(queues) + ["net"]}
+    ready = {e: [] for e in free}
+    for o in ops:
+        if not left[o["i"]]:
+            ready[o["e"]].append((0.0, o))
+    done = []
+    while len(done) < len(ops):
+        best = None
+        for e in ready:
+            for (r, o) in ready[e]:
+                k = (max(r, free[e] if e != "net" else 0.0), -o["pri"], o["i"])
+                if best is None or k < best[0]:
+                    best = (k, e, r, o)
+        k, e, r, o = best
+        ready[e].remove((r, o))
+        o["st"] = k[0]
+        o["fin"] = k[0] + o["cost"] + o["lat"]
+        free[e] = k[0] + o["cost"]
+        done.append(o)
+        for s in succ[o["i"]]:
+            left[s["i"]] -= 1
+            if not left[s["i"]]:
+                ready[s["e"]].append((max([x["fin"] + WK for x in s["need"]] + [x["fin"] for x in s["soft"]]), s))
+    count = {}
+    clock = {e: {} for e in queues}
+    for o in done:
+        e = o["e"]
+        if e == "net":
+            o["c"] = {}
+            continue
+        want = {}
+        for x in o["need"]:
+            if x["v"] > want.get(x["sem"], (0, None))[0]:
+                want[x["sem"]] = (x["v"], x)
+        ck = clock[e]
+        for s in sorted(want, key=lambda s: -len(want[s][1]["c"])):
+            v, x = want[s]
+            if ck.get(s, 0) >= v:
+                continue
+            queues[e].wait_ge(T.sem[s], v)
+            for k, y in x["c"].items():
+                ck[k] = max(ck.get(k, 0), y)
+            ck[s] = v
+        ins = o["fn"](queues[e])
+        if o["inc"] > 0:
+            ins.then_inc(T.sem[o["sem"]], o["inc"])
+        count[o["sem"]] = count.get(o["sem"], 0) + abs(o["inc"])
+        o["v"] = count[o["sem"]]
+        o["c"] = dict(ck)
     for s in sorted(count):
-        if count[s] and clock["g"].get(s, 0) < count[s]:
+        if clock["g"].get(s, 0) < count[s]:
             g.wait_ge(T.sem[s], count[s])

@@ -18,10 +18,10 @@ for _n, _w, _d in (
         ("Z1", 144, BF), ("ZL", 144, BF), ("ZC", 144, BF), ("ZS", 144, BF), ("GW", 128, BF), ("BO", 128, BF), ("EY", 128, BF), ("NE", 128, BF),
         ("PM", Q, BF), ("S00", 128, F32), ("S01", 128, F32), ("S10", 128, F32), ("S11", 128, F32),
         ("pI", Q, I32), ("qI", Q, I32), ("kI", Q, I32), ("nI", 144, I32), ("mpI", 128, I32), ("c16I", Q, I32),
-        ("k1", Q, I32), ("k2", Q, I32), ("k3", Q, F32), ("k4", Q, F32), ("k5", 128, I32), ("k6", 128, I32), ("k7", 128, I32), ("k8", 12, I32), ("k9", 144, I32), ("k10", 144, I32),
         ("b4", 8, I32), ("bF", 8, F32), ("cF", 48, F32), ("c256", 12, I32),
-        ("X0", 384, F32), ("X1", 384, F32), ("M0", 384, F32), ("M1", 384, F32), ("T0", 448, F32), ("T1", 448, F32), ("E0", 384, F32), ("oB", 384, BF),
-        ("tA", Q, F32), ("tB", Q, F32), ("tC", Q, F32), ("tD", Q, F32), ("tE", Q, F32), ("tF", Q, I32),
+        ("X0", 384, F32), ("X1", 384, BF), ("ML0", Q, F32), ("ML1", Q, F32), ("MV0", Q, F32), ("MV1", Q, F32), ("MO0", 384, BF), ("MO1", 384, BF),
+        ("TL0", 256, F32), ("TL1", 256, F32), ("TV0", 256, F32), ("TV1", 256, F32), ("TO0", 448, BF), ("TO1", 448, BF), ("E0", 384, F32), ("oB", 384, BF),
+        ("B00", 128, BF), ("B01", 128, BF), ("B10", 128, BF), ("B11", 128, BF), ("KX", 1072, I32), ("TX", 7 * Q, F32), ("tF", Q, I32),
         ("y_", Q, F32), ("KEYC", Q, F32), ("SLT", Q, F32), ("tS", Q, I32), ("mkL", Q, F32), ("mk", Q, F32), ("hot", Q, F32),
         ("RLS", 384, F32), ("RC", Q, F32), ("bL", Q, F32), ("bR", Q, F32), ("bN", Q, F32),
         ("dif", Q, F32), ("sL", Q, I32), ("sM", Q, I32), ("sC", Q, I32), ("LI", 312, I32), ("LF", 480, F32), ("Bf", 12, BF), ("LST", 24, U16),
@@ -41,7 +41,10 @@ for _t in range(TV):
         SCRATCH["aV%d" % _t] = ("sbuf", [128, 2 * Q], I32)
 SEMAPHORES = ["sv", "ss", "st", "sg"] + [k + i for k in ("lL", "lC", "lV") for i in "01"] + ["d%d" % i for i in range(16)] + [k + "%d" % t for k in ("qL", "qC", "qV") for t in range(1, TV)]
 PART = {"cv": ("cF", 0, 12), "cp": ("cF", 12, 12), "cb": ("cF", 24, 24),
-        "u": ("XS", 192, 12), "w": ("XS", 208, 12), "lm": ("XS", 224, 192), "RL": ("RLS", 0, 192), "RS": ("RLS", 192, 192)}
+        "k1": ("KX", 0, Q), "k2": ("KX", Q, Q), "k5": ("KX", 384, 128), "k6": ("KX", 512, 128), "k7": ("KX", 640, 128), "k8": ("KX", 768, 12),
+        "k9": ("KX", 784, 144), "k10": ("KX", 928, 144), "tA": ("TX", 0, Q), "tB": ("TX", Q, Q), "tC": ("TX", 2 * Q, Q), "tD": ("TX", 3 * Q, Q),
+        "tE": ("TX", 4 * Q, Q), "k3": ("TX", 5 * Q, Q), "k4": ("TX", 6 * Q, Q),
+        "u": ("XC", 192, 12), "w": ("XC", 208, 12), "lm": ("XC", 224, 192), "RL": ("RLS", 0, 192), "RS": ("RLS", 192, 192)}
 BONUS = 4.0
 CY, FX, WK = 0.00092, 0.03, 0.08
 
@@ -183,9 +186,10 @@ def rank_program(g, core, T, topo):
     iota(A("c16I"), [[16, 12], [0, 16]], 0, 0)
     iota(A("c256"), [[256, 12]], 0, 0)
     iota(A("KT"), [[0, 12], [-1, 16]], 15, 0)
-    for x in ("T0", "T1"):
+    for x in ("TL0", "TL1", "TV0", "TV1", "TO0", "TO1"):
+        n = SCRATCH[x][1][1]
         iota(A(x, 0, 32), [[0, 32]], 0, 0)
-        iota(A(x, 416, 448), [[0, 32]], 0, 0)
+        iota(A(x, n - 32, n), [[0, 32]], 0, 0)
     iota(A("P", W, PW), [[0, PW - W]], 0, 0)
     iota(A("D", NPOS, NPOS + Q), [[0, Q]], 0, 0)
     for x in ("bL", "bR", "bN"):
@@ -200,32 +204,35 @@ def rank_program(g, core, T, topo):
     ts(A("S01"), A("mpI"), 16, op.is_equal, b0, op.mult)
     ts(A("S10"), A("mpI"), -16, op.is_equal, b1, op.mult)
 
-    def turn(x):
-        act(A("M0"), x, af.Copy, scale=b0)
-        act(A("M1"), x, af.Copy, scale=b1)
-        vtr(A("T0", 32, 416), A("M0"))
-        vtr(A("T1", 32, 416), A("M1"))
-        mms(A("SWP", 0, 384), [(A("S00"), A("T0", 32, 416)), (A("S11"), A("T1", 32, 416)), (A("S01"), A("T1", 48, 432)), (A("S10"), A("T0", 16, 400))])
+    def turn(x, m, t, s, out):
+        n = x[4]
+        for j, b in ((0, b0), (1, b1)):
+            act(A(m + "%d" % j, 0, n), x, af.Copy, scale=b)
+            vtr(A(t + "%d" % j, 32, 32 + n), A(m + "%d" % j, 0, n))
+        mms(out, [(A(s + "00"), A(t + "0", 32, 32 + n)), (A(s + "11"), A(t + "1", 32, 32 + n)), (A(s + "01"), A(t + "1", 48, 48 + n)), (A(s + "10"), A(t + "0", 16, 16 + n))])
 
     act(A("XL", 0, Q), A("inO"), af.Copy, scale=-16384.0, bias=15 * 16384.0)
     act(A("XC", 0, Q), A("inB"), af.Copy, scale=262144.0)
     act(A("OB", 0, Q), A("inB"), af.Copy, scale=2.0 - 262144.0, bias=2105344.0)
     cp(A("X0", 0, Q), A("inL"))
+    turn(A("X0", 0, Q), "ML", "TL", "S", A("SWP", 0, Q))
     ts(A("tB"), A("inC"), 0, op.max, 2, op.mult)
     ts(A("tD"), A("inC"), 0, op.is_lt)
     tt(A("tA"), A("XL", 0, Q), A("tB"), op.add)
     tt(A("tC"), A("XC", 0, Q), A("tA"), op.add)
     tt(A("tE"), A("OB", 0, Q), A("tD"), op.mult)
     tt(A("X0", Q, 2 * Q), A("tC"), A("tE"), op.add)
-    turn(A("X0"))
+    turn(A("X0", Q, 2 * Q), "MV", "TV", "S", A("OB", 0, Q))
     K13, K21 = A("VP1", 0, Q), A("VP1", Q, 2 * Q)
     KC, TH = A("VP2", 0, Q), A("VP2", Q, 2 * Q)
     TA, TB = A("VT", 0, Q), A("VT", Q, 2 * Q)
     ts(K13, kI, -8192, op.mult, 4096 + 15 * 8192, op.add)
     cp(A("oL0"), A("SWP", 0, Q))
-    act(A("X1", 0, Q), A("SWP", 0, Q), af.Copy)
-    cp(A("oV0", Q, 2 * Q), A("SWP", Q, 2 * Q))
-    tt(A("oV0", 0, Q), A("X1", 0, Q), K13, op.add)
+    act(A("E0", 0, Q), A("SWP", 0, Q), af.Copy)
+    cp(A("oV0", Q, 2 * Q), A("OB", 0, Q))
+    tt(A("oV0", 0, Q), A("E0", 0, Q), K13, op.add)
+    for x in ("00", "01", "10", "11"):
+        act(A("B" + x), A("S" + x), af.Copy)
 
     def coff(t):
         ts(A("sC"), A("oV%d" % (t % 2), Q, 2 * Q), 1, op.arith_shift_right, 8191, op.bitwise_and)
@@ -318,6 +325,8 @@ def rank_program(g, core, T, topo):
         mms(A("u"), [(A("Z1", 15 - q, 143 - q), A("AB%d" % p, NPOS + q, NPOS + Q, 16)) for q in range(16)])
         act(LF(36), A("u"), af.Copy)
         act(LF(37), A("u"), af.Copy)
+
+    def uint():
         return cp(LI(2), LF(36))
 
     def wcount(t):
@@ -337,6 +346,7 @@ def rank_program(g, core, T, topo):
         return A(name, a, None, 16) if name not in PART else A(name, a, PART[name][2], 16)
 
     lims(0)
+    usum(0)
     for t in range(TV):
         p = t % 2
         AB, yv = A("AB%d" % p), A("AB%d" % p, NPOS, NPOS + Q)
@@ -347,7 +357,7 @@ def rank_program(g, core, T, topo):
         seq = gather_l(t)
         wseq = wcount(t) if t else [scan(TH, A("MSK"), A("DL0"), 0.0, op.mult, op.add)]
         seq += gather_c(t)
-        seq.append(usum(p))
+        seq.append(uint())
         wseq[0]["soft"].append(seq[0])
         chain(seq)
         gather_s(t)
@@ -356,8 +366,6 @@ def rank_program(g, core, T, topo):
         ts(A("tS"), V, 15 << 18, op.bitwise_and, 9, op.arith_shift_right)
         tt(A("KEYC"), A("y_"), K21, op.add)
         tt(A("SLT"), A("tS"), KC, op.add)
-        if not last:
-            lims(nxt)
         tt(A("mkL"), A("XL", 0, Q), Lp, op.min)
         scan(A("RS"), A("RSTL"), A("XS", 0, Q), -2.0 ** 20, op.min, op.max)
         scan(A("RL"), A("RSTL"), A("mkL"), -2.0 ** 20, op.min, op.max)
@@ -388,6 +396,8 @@ def rank_program(g, core, T, topo):
         tt(TA, A("XC", 0, Q), A("KEYC"), op.min)
         tt(A("mk"), TA, A("SLT"), op.max)
         scan(A("RC"), A("RSTC"), A("mk"), -2.0 ** 27, op.min, op.max)
+        if not last:
+            lims(nxt)
         cp(LI(16), RC)
         ts(LF(14), RC, -2.0 ** 24, op.is_lt)
         ts(LF(15), RC, -2.0 ** 24, op.is_ge)
@@ -442,27 +452,30 @@ def rank_program(g, core, T, topo):
         yexp(1 - p)
         cp(A("Bf"), LF(15))
         mms(A("w"), [(A("GW"), A("Bf"))])
+        usum(1 - p)
 
     dma("y", T.zp[:, :], T.P[:, 0:W], [A("P", 0, W)], [], 6.0)
     pe = TV % 2
     dma("y", T.zy[:, :], T["AB%d" % pe][:, NPOS:NPOS + Q], [A("AB%d" % pe, NPOS, NPOS + Q)], [], 2.0)
     VN = A("oV%d" % pe, Q, 2 * Q)
     cp(A("X0", 0, Q), A("sM"))
+    turn(A("X0", 0, Q), "ML", "TL", "S", A("SWP", 0, Q))
+    act(A("E0", 0, Q), A("SWP", 0, Q), af.Copy)
+    dma("y", T.zl[:, :], T.E0[:, 0:Q], [A("E0", 0, Q)], [], 2.0)
     ts(A("tF"), VN, 1, op.arith_shift_right, 8191, op.bitwise_and)
     ts(A("tA"), A("tF"), 4096, op.is_lt)
     ts(TB, A("tF"), 1, op.add)
     tt(A("tC"), A("tA"), TB, op.mult)
     ts(A("X0", Q, 2 * Q), A("tC"), -1, op.add)
-    turn(A("X0"))
+    turn(A("X0", Q, 2 * Q), "MV", "TV", "S", A("OB", 0, Q))
     ts(A("sL"), VN, 14, op.arith_shift_right, 15, op.bitwise_and)
     ts(A("X1", 0, Q), A("sL"), -1, op.mult, 15, op.add)
     ts(A("sC"), VN, 18, op.arith_shift_right, 7, op.bitwise_and)
     ts(TB, A("tF"), -4096, op.add, 0, op.max)
     tt(A("X1", Q, 2 * Q), A("sC"), TB, op.add)
-    act(A("E0"), A("SWP", 0, 384), af.Copy)
-    dma("y", T.zl[:, :], T.E0[:, 0:Q], [A("E0", 0, Q)], [], 2.0)
+    act(A("E0", Q, 2 * Q), A("OB", 0, Q), af.Copy)
     dma("y", T.zc[:, :], T.E0[:, Q:2 * Q], [A("E0", Q, 2 * Q)], [], 2.0)
-    turn(A("X1"))
+    turn(A("X1"), "MO", "TO", "B", A("SWP", 0, 384))
     act(A("oB"), A("SWP", 0, 384), af.Copy)
     dma("y", T.zo[:, :], T.oB[:, 0:Q], [A("oB", 0, Q)], [], 2.0)
     dma("y", T.zb[:, :], T.oB[:, Q:2 * Q], [A("oB", Q, 2 * Q)], [], 2.0)

from concourse.mybir import AluOpType, ActivationFunctionType

N, W, Q, TV, HOP = 8, 4096, 192, 6, 3
NPOS = 16 * Q
PW = 4608
DUMP = 4352
LCH = [(0, 64), (64, 128), (128, 192)]
CCH = [(0, 64), (64, 128)]
SCH = [(128, 160), (160, 192)]

F32, BF, I32, U16 = "float32", "bfloat16", "int32", "uint16"
SCRATCH = {}
for _n, _w, _d in (
        ("P", PW, BF), ("D", NPOS + Q, BF), ("AB0", NPOS + Q, BF), ("AB1", NPOS + Q, BF), ("SG", NPOS, BF), ("IC", NPOS, BF),
        ("YE", NPOS, BF), ("CR", NPOS, BF), ("YL", Q, U16),
        ("inL", Q, I32), ("inC", Q, I32), ("inO", Q, BF), ("inB", Q, BF), ("inLim", 8, I32), ("limF", 8, F32),
        ("MSK", Q, F32), ("RSTL", Q, F32), ("RSTC", Q, F32), ("KT", Q, BF), ("CL", Q, BF), ("CC", Q, BF), ("ONE", 128, BF),
        ("Z1", 144, BF), ("ZL", 144, BF), ("ZC", 144, BF), ("ZS", 144, BF), ("GW", 128, BF), ("BO", 128, BF), ("EY", 128, BF), ("NE", 128, BF),
        ("PM", Q, BF), ("S00", 128, F32), ("S01", 128, F32), ("S10", 128, F32), ("S11", 128, F32),
        ("pI", Q, I32), ("qI", Q, I32), ("kI", Q, I32), ("nI", 144, I32), ("mpI", 128, I32), ("c16I", Q, I32),
        ("b4", 8, I32), ("bF", 8, F32), ("cF", 48, F32), ("c256", 12, I32),
        ("X0", 384, F32), ("X1", 384, BF), ("ML0", Q, F32), ("ML1", Q, F32), ("MV0", Q, F32), ("MV1", Q, F32), ("MO0", 384, BF), ("MO1", 384, BF),
        ("TL0", 256, F32), ("TL1", 256, F32), ("TV0", 256, F32), ("TV1", 256, F32), ("TO0", 448, BF), ("TO1", 448, BF), ("E0", 384, F32), ("oB", 384, BF),
        ("B00", 128, BF), ("B01", 128, BF), ("B10", 128, BF), ("B11", 128, BF), ("KX", 1072, I32), ("TX", 7 * Q, F32), ("tF", Q, I32),
        ("y_", Q, F32), ("KEYC", Q, F32), ("SLT", Q, F32), ("tS", Q, I32), ("mkL", Q, F32), ("mk", Q, F32), ("hot", Q, F32),
        ("RLS", 384, F32), ("RC", Q, F32), ("bL", Q, F32), ("bR", Q, F32), ("bN", Q, F32),
        ("dif", Q, F32), ("sL", Q, I32), ("sM", Q, I32), ("sC", Q, I32), ("LI", 312, I32), ("LF", 480, F32), ("Bf", 12, BF), ("LST", 24, U16),
        ("md", Q, BF), ("nD", Q, BF)):
    SCRATCH[_n] = ("sbuf", [128, _w], _d)
for _n in ("XL", "XS", "XC", "VP1", "VP2", "VT", "OB", "SWP"):
    SCRATCH[_n] = ("psum", [128, 512], F32)
for _t in range(TV):
    SCRATCH["PM1_%d" % (_t % 2)] = ("sbuf", [128, Q], BF)
    SCRATCH["DL%d" % (_t % 2)] = ("sbuf", [128, Q], F32)
    SCRATCH["oL%d" % (_t % 2)] = ("sbuf", [128, Q], U16)
    SCRATCH["oC%d" % (_t % 2)] = ("sbuf", [128, Q], U16)
    SCRATCH["oV%d" % (_t % 2)] = ("sbuf", [128, 2 * Q], I32)
    if _t:
        SCRATCH["aL%d" % _t] = ("sbuf", [128, Q], U16)
        SCRATCH["aC%d" % _t] = ("sbuf", [128, Q], U16)
        SCRATCH["aV%d" % _t] = ("sbuf", [128, 2 * Q], I32)
SEMAPHORES = ["sv", "ss", "st", "sg"] + [k + i for k in ("lL", "lC", "lV") for i in "01"] + ["d%d" % i for i in range(16)] + [k + "%d" % t for k in ("qL", "qC", "qV") for t in range(1, TV)]
PART = {"cv": ("cF", 0, 12), "cp": ("cF", 12, 12), "cb": ("cF", 24, 24),
        "k1": ("KX", 0, Q), "k2": ("KX", Q, Q), "k5": ("KX", 384, 128), "k6": ("KX", 512, 128), "k7": ("KX", 640, 128), "k8": ("KX", 768, 12),
        "k9": ("KX", 784, 144), "k10": ("KX", 928, 144), "tA": ("TX", 0, Q), "tB": ("TX", Q, Q), "tC": ("TX", 2 * Q, Q), "tD": ("TX", 3 * Q, Q),
        "tE": ("TX", 4 * Q, Q), "k3": ("TX", 5 * Q, Q), "k4": ("TX", 6 * Q, Q),
        "u": ("XC", 192, 12), "w": ("XC", 208, 12), "lm": ("XC", 224, 192), "RL": ("RLS", 0, 192), "RS": ("RLS", 192, 192)}
BONUS = 4.0
CY, FX, WK = 0.00092, 0.03, 0.08


def rank_program(g, core, T, topo):
    rank = T.rank_of(core)
    if rank is None:
        return
    dst = T.cores[(rank + HOP) % N]
    rid, pid = topo.addr(dst)[:2]
    emask = topo.mask(core, dst)
    neng = len(topo.engines(core, dst))
    op = AluOpType
    af = ActivationFunctionType
    queues = {"v": g.vector, "s": g.scalar, "t": g.tensor, "g": g, "y": g.sync}
    semof = {"v": "sv", "s": "ss", "t": "st", "g": "sg"}
    ops, wr, rd = [], {}, {}
    psum = {k for k in SCRATCH if SCRATCH[k][0] == "psum"}

    def A(name, lo=0, hi=None, st=1):
        if name in PART:
            name, base, n = PART[name]
            lo, hi = base + lo, base + (n if hi is None else hi)
        hi = SCRATCH[name][1][1] if hi is None else hi
        return (name, lo, hi, T[name][:, lo:hi] if st == 1 else T[name][:, lo:hi:st], len(range(lo, hi, st)))

    def emit(e, fn, R, Wt, cost, sem=None, inc=1, lat=0.0, deps=()):
        need = list(deps)
        for x in R:
            for (l, h, o) in wr.get(x[0], []):
                if (l < x[2] and x[1] < h) or (x[0] in psum and o["e"] != e):
                    need.append(o)
            if x[0] in psum:
                need += [o for (l, h, o) in rd.get(x[0], []) if o["e"] != e]
        for x in Wt:
            for (l, h, o) in wr.get(x[0], []) + rd.get(x[0], []):
                if (l < x[2] and x[1] < h) or (x[0] in psum and o["e"] != e):
                    need.append(o)
        me = {"e": e, "fn": fn, "need": need, "cost": cost, "sem": sem or semof.get(e), "inc": inc, "lat": lat, "i": len(ops), "soft": [], "bonus": 0.0}
        ops.append(me)
        for x in R:
            rd.setdefault(x[0], []).append((x[1], x[2], me))
        for x in Wt:
            nm, lo, hi = x[:3]
            wr[nm] = [y for y in wr.get(nm, []) if not (lo <= y[0] and y[1] <= hi)] + [(lo, hi, me)]
            rd[nm] = [y for y in rd.get(nm, []) if not (lo <= y[0] and y[1] <= hi) or y[2] is me]
        return me

    def two(x):
        return SCRATCH[x[0]][2] in (BF, U16)

    def vc(o, ins):
        n = max([x[4] for x in [o] + ins])
        return FX + CY * max(64, n * (0.5 if all(two(x) for x in [o] + ins) else 1))

    def ts(o, i, s1, op0, s2=None, op1=None):
        if op1 is None:
            return emit("v", lambda q: q.tensor_scalar(o[3], i[3], s1, None, op0), [i], [o], vc(o, [i]))
        sc = s2[3] if isinstance(s2, tuple) else s2
        return emit("v", lambda q: q.tensor_scalar(o[3], i[3], s1, sc, op0, op1), [i] + ([s2] if isinstance(s2, tuple) else []), [o], vc(o, [i]))

    def tt(o, a, b, o_):
        k = 1 if a[0] in psum or b[0] in psum else 2
        return emit("v", lambda q: q.tensor_tensor(o[3], a[3], b[3], o_), [a, b], [o], FX + CY * max(64, k * o[4]))

    def cp(o, i):
        return emit("v", lambda q: q.tensor_copy(o[3], i[3]), [i], [o], vc(o, [i]))

    def fill(o, c):
        return emit("v", lambda q: q.memset(o[3], c), [], [o], vc(o, []))

    def scan(o, d0, d1, init, p0, p1):
        return emit("v", lambda q: q.tensor_tensor_scan(o[3], d0[3], d1[3], init, p0, p1), [d0, d1], [o], vc(o, [d0, d1]))

    def vtr(o, i):
        return emit("v", lambda q: q.transpose(o[3], i[3]), [i], [o], vc(o, [i]))

    def act(o, i, f, bias=0.0, scale=1.0, off=None):
        src = i[3].indirect(off[3]) if off else i[3]
        f = af.Identity if f == af.Copy and bias else f
        sc, extra = (scale[3], [scale]) if isinstance(scale, tuple) else (scale, [])
        return emit("s", lambda q: q.activation(o[3], src, f, bias=bias, scale=sc), [i] + ([off] if off else []) + extra, [o],
                    (0.065 + 1.56 * CY * o[4]) if off else FX + CY * max(64, o[4]))

    def pool(o, fn):
        return emit("g", fn, [], [o], 0.13 + 2 * CY * o[4])

    def iota(o, pattern, base, cm):
        if SCRATCH[o[0]][2] == I32:
            return pool(o, lambda q: q.iota(o[3], pattern, base, cm))
        return pool(o, lambda q: q.iota(o[3], pattern, base, cm, allow_small_or_imprecise_dtypes=True))

    def mms(o, terms):
        R = [x for t in terms for x in t]

        def go(q):
            for j, (l, r) in enumerate(terms):
                ins = q.matmul(o[3], l[3], r[3], j == 0, j == len(terms) - 1)
            return ins
        k = 4 if SCRATCH[terms[0][0][0]][2] == F32 else 1
        return emit("t", go, R, [o], FX + 0.00078 * k * max(64, o[4]) * len(terms))

    nd = [0]

    def dma(e, o, i, R, Wt, lat):
        s = "d%d" % nd[0]
        nd[0] += 1
        return emit(e, lambda q: q.dma_start(o, i), R, Wt, 0.05, sem=s, inc=16, lat=lat)

    def LI(j, n=1):
        return A("LI", 12 * j, 12 * (j + n))

    def LF(j, n=1):
        return A("LF", 12 * j, 12 * (j + n))

    def send(k, nxt):
        o, i = "a%s%d" % (k, nxt), "o%s%d" % (k, nxt % 2)
        sl = "l%s%d" % (k, nxt % 2)
        wid = SCRATCH[o][1][1]
        lat = 1.6 + 128 * wid * (2 if k != "V" else 4) / 60e3
        me = emit("g", lambda q: q.remote_dma(out_ap=T[o][:, :], in_ap=T[i][:, :], remote_sem=T.sem["q%s%d" % (k, nxt)], local_sem=T.sem[sl],
                                              pid=pid, routing_id=rid, dma_engine_mask=emask), [A(i)], [], 0.6, sem=sl, inc=-neng, lat=lat)
        net = {"e": "net", "need": [me], "cost": lat, "sem": "q%s%d" % (k, nxt), "v": neng, "inc": 0, "lat": 0.0, "i": len(ops), "soft": [], "bonus": 0.0}
        ops.append(net)
        wr[o] = [(0, wid, net)]

    dma("y", T.inC[:, :], T.con[:, :], [], [A("inC")], 2.0)
    dma("y", T.inO[:, :], T.org[:, :], [], [A("inO")], 2.0)
    dma("s", T.inB[:, :], T.cnt[:, :], [], [A("inB")], 2.0)
    dma("y", T.inL[:, :], T.lem[:, :], [], [A("inL")], 2.2)
    dma("s", T.AB0[:, NPOS:NPOS + Q], T.ex[:, :], [], [A("AB0", NPOS, NPOS + Q)], 2.2)
    dma("y", T.inLim[:, 0:TV], T.lim[:, :], [], [A("inLim", 0, TV)], 2.2)
    dma("y", T.P[:, 0:W], T.prop[:, :], [], [A("P", 0, W)], 6.0)

    iota(A("mpI"), [[1, 128]], 0, -1)
    iota(A("pI"), [[0, Q]], 0, 1)
    iota(A("kI"), [[0, 12], [1, 16]], 0, 0)
    iota(A("nI"), [[1, 144]], 0, 0)
    iota(A("c16I"), [[16, 12], [0, 16]], 0, 0)
    iota(A("c256"), [[256, 12]], 0, 0)
    iota(A("KT"), [[0, 12], [-1, 16]], 15, 0)
    for x in ("TL0", "TL1", "TV0", "TV1", "TO0", "TO1"):
        n = SCRATCH[x][1][1]
        iota(A(x, 0, 32), [[0, 32]], 0, 0)
        iota(A(x, n - 32, n), [[0, 32]], 0, 0)
    iota(A("P", W, PW), [[0, PW - W]], 0, 0)
    iota(A("D", NPOS, NPOS + Q), [[0, Q]], 0, 0)
    for x in ("bL", "bR", "bN"):
        iota(A(x), [[0, Q]], 0, 0)
    kI = A("kI")
    b0, b1 = A("bF", 0, 1), A("bF", 1, 2)
    ts(A("b4", 0, 1), A("pI", 0, 1), 16, op.bitwise_and)
    ts(b0, A("b4", 0, 1), 0, op.is_equal)
    ts(b1, A("b4", 0, 1), 16, op.is_equal)
    ts(A("S00"), A("mpI"), 0, op.is_equal, b0, op.mult)
    ts(A("S11"), A("mpI"), 0, op.is_equal, b1, op.mult)
    ts(A("S01"), A("mpI"), 16, op.is_equal, b0, op.mult)
    ts(A("S10"), A("mpI"), -16, op.is_equal, b1, op.mult)

    def turn(x, m, t, s, out):
        n = x[4]
        for j, b in ((0, b0), (1, b1)):
            act(A(m + "%d" % j, 0, n), x, af.Copy, scale=b)
            vtr(A(t + "%d" % j, 32, 32 + n), A(m + "%d" % j, 0, n))
        mms(out, [(A(s + "00"), A(t + "0", 32, 32 + n)), (A(s + "11"), A(t + "1", 32, 32 + n)), (A(s + "01"), A(t + "1", 48, 48 + n)), (A(s + "10"), A(t + "0", 16, 16 + n))])

    act(A("XL", 0, Q), A("inO"), af.Copy, scale=-16384.0, bias=15 * 16384.0)
    act(A("XC", 0, Q), A("inB"), af.Copy, scale=262144.0)
    act(A("OB", 0, Q), A("inB"), af.Copy, scale=2.0 - 262144.0, bias=2105344.0)
    cp(A("X0", 0, Q), A("inL"))
    turn(A("X0", 0, Q), "ML", "TL", "S", A("SWP", 0, Q))
    ts(A("tB"), A("inC"), 0, op.max, 2, op.mult)
    ts(A("tD"), A("inC"), 0, op.is_lt)
    tt(A("tA"), A("XL", 0, Q), A("tB"), op.add)
    tt(A("tC"), A("XC", 0, Q), A("tA"), op.add)
    tt(A("tE"), A("OB", 0, Q), A("tD"), op.mult)
    tt(A("X0", Q, 2 * Q), A("tC"), A("tE"), op.add)
    turn(A("X0", Q, 2 * Q), "MV", "TV", "S", A("OB", 0, Q))
    K13, K21 = A("VP1", 0, Q), A("VP1", Q, 2 * Q)
    KC, TH = A("VP2", 0, Q), A("VP2", Q, 2 * Q)
    TA, TB = A("VT", 0, Q), A("VT", Q, 2 * Q)
    ts(K13, kI, -8192, op.mult, 4096 + 15 * 8192, op.add)
    cp(A("oL0"), A("SWP", 0, Q))
    act(A("E0", 0, Q), A("SWP", 0, Q), af.Copy)
    cp(A("oV0", Q, 2 * Q), A("OB", 0, Q))
    tt(A("oV0", 0, Q), A("E0", 0, Q), K13, op.add)
    for x in ("00", "01", "10", "11"):
        act(A("B" + x), A("S" + x), af.Copy)

    def coff(t):
        ts(A("sC"), A("oV%d" % (t % 2), Q, 2 * Q), 1, op.arith_shift_right, 8191, op.bitwise_and)
        cp(A("oC%d" % (t % 2)), A("sC"))
    coff(0)
    ts(A("qI"), A("pI"), 15, op.bitwise_and)
    tt(A("k1"), A("c16I"), A("qI"), op.add)
    cp(A("YL"), A("k1"))

    def chain(seq):
        for x, y in zip(seq, seq[1:]):
            y["soft"].append(x)

    def yexp(p):
        seq = [act(A("YE", 16 * a, 16 * b), A("AB%d" % p, NPOS, NPOS + Q), af.Copy, off=A("YL", a, b)) for a, b in LCH]
        chain(seq)
        seq[0]["bonus"] = BONUS
    yexp(0)
    ts(A("k9"), A("pI", 0, 144), 240, op.bitwise_and)
    tt(A("k10"), A("nI"), A("k9"), op.subtract)
    ts(A("Z1"), A("k10"), 15, op.is_equal)
    for z, s in (("ZL", 2.0 ** 25), ("ZS", -16.0), ("ZC", 2.0 ** 26)):
        act(A(z), A("Z1"), af.Copy, scale=s)
    ts(A("EY"), A("mpI"), 0, op.is_equal)
    act(A("NE"), A("EY"), af.Copy, scale=-1.0)
    fill(A("ONE"), 1.0 / 128)
    fill(A("CL"), 2.0 ** 25)
    fill(A("CC"), -7.5 * 2.0 ** 26)
    ts(A("MSK"), kI, 0, op.is_gt)
    ts(K21, kI, -(1 << 21), op.mult, 15 * (1 << 21) - (1 << 24) + (1 << 13), op.add)
    ts(KC, kI, -2, op.mult, 30 - (1 << 24) - (1 << 13), op.add)
    act(A("RSTL"), A("MSK"), af.Copy, scale=2.0 ** 27, bias=-2.0 ** 20)
    act(A("RSTC"), A("MSK"), af.Copy, scale=2.0 ** 28, bias=-2.0 ** 27)
    cp(A("limF", 0, TV), A("inLim", 0, TV))
    tt(A("k2"), kI, A("qI"), op.subtract)
    ts(A("k3"), A("k2"), 0, op.is_equal)
    ts(A("k4"), A("k2"), 1, op.is_equal)
    tt(A("PM"), A("k3"), A("k4"), op.subtract)
    ts(A("k5"), A("nI", 0, 128), 240, op.bitwise_and)
    ts(A("k6"), A("pI", 0, 128), 240, op.bitwise_and)
    tt(A("BO"), A("k5"), A("k6"), op.is_equal)
    ts(A("k7"), A("mpI"), 15, op.bitwise_and)
    ts(A("GW"), A("k7"), 0, op.is_equal, 2.0 ** 18, op.mult)
    tt(A("k8"), A("c16I", 0, Q, 16), A("qI", 0, 12), op.add)
    cp(A("cv"), A("k8"))
    ts(A("cb", 0, 12), A("k8"), NPOS, op.add)
    ts(A("cb", 12, 24), A("k8"), DUMP, op.add)
    tt(A("tA", 0, 12), A("c256"), A("qI", 0, 12), op.add)
    ts(A("tB", 0, 12), A("tA", 0, 12), 240, op.add)
    tt(A("cp"), A("tB", 0, 12), A("cb", 0, 12), op.subtract)

    def cnt(x, src, z, const, a, b):
        mms(A(x, a, b), [(A("ONE"), A(const, a, b))] + [(A(z, 15 - q, 143 - q), A(src, a * 16 + q, b * 16, 16)) for q in range(16)])

    def gather_l(t):
        lst, ab = ("aL%d" if t else "oL%d") % t, "AB%d" % (t % 2)

        def one(a, b):
            off, ye, o = A(lst, a, b), A("YE", 16 * a, 16 * b), A("D", 16 * a, 16 * b)
            me = emit("v", lambda q: q.tensor_tensor(o[3], T.P[:, :].indirect(off[3]), ye[3], op.subtract), [A("P"), off, ye], [o], 0.05 + 1.56 * CY * o[4])
            act(A("SG", 16 * a, 16 * b), o, af.Sign, bias=-0.5)
            act(A(ab, 16 * a, 16 * b), o, af.Abs)
            cnt("XL", "SG", "ZL", "CL", a, b)
            cnt("XS", ab, "ZS", "KT", a, b)
            return me
        return [one(a, b) for a, b in LCH]

    def gather_c(t):
        lst = ("aC%d" if t else "oC%d") % t

        def one(a, b):
            off, ye, o = A(lst, a, b), A("YE", 16 * a, 16 * b), A("IC", 16 * a, 16 * b)
            me = emit("v", lambda q: q.tensor_tensor(o[3], T.P[:, :].indirect(off[3]), ye[3], op.is_gt), [A("P"), off, ye], [o], 0.05 + 1.56 * CY * o[4])
            cnt("XC", "IC", "ZC", "CC", a, b)
            return me
        return [one(a, b) for a, b in CCH]

    def gather_s(t):
        lst = ("aC%d" if t else "oC%d") % t
        for a, b in SCH:
            act(A("CR", 16 * a, 16 * b), A("P"), af.Copy, off=A(lst, a, b))
        for j, (a, b) in enumerate(SCH):
            ps = A(("OB", "SWP")[j % 2], 0, 16 * (b - a))
            mms(ps, [(A("EY"), A("CR", 16 * a, 16 * b)), (A("NE"), A("YE", 16 * a, 16 * b))])
            act(A("IC", 16 * a, 16 * b), ps, af.Sign, bias=-0.5)
        if SCH:
            cnt("XC", "IC", "ZL", "CL", SCH[0][0], SCH[-1][1])

    def usum(p):
        mms(A("u"), [(A("Z1", 15 - q, 143 - q), A("AB%d" % p, NPOS + q, NPOS + Q, 16)) for q in range(16)])
        act(LF(36), A("u"), af.Copy)
        act(LF(37), A("u"), af.Copy)

    def uint():
        return cp(LI(2), LF(36))

    def wcount(t):
        d = "DL%d" % (t % 2)
        return [cp(LI(21), A("w")), ts(LI(22), LI(21), 3 << 18, op.bitwise_and), tt(starts(d, 0), starts(d, 0), LI(22), op.add),
                scan(TH, A("MSK"), A(d), 0.0, op.mult, op.add)]

    def lims(t):
        act(A("PM1_%d" % (t % 2)), A("PM"), af.Copy, scale=A("limF", t, t + 1))
        mms(A("lm"), [(A("BO"), A("PM1_%d" % (t % 2)))])
        act(A("DL%d" % (t % 2)), A("lm"), af.Copy, scale=2.0 ** 18)

    def pnew(to, y):
        return emit("v", lambda q: q.tensor_tensor(T.P[:, :].indirect(to[3]), T.md[:, :], y[3], op.add), [A("md"), y, to], [A("P")], 0.05 + 3.8 * CY * Q)

    def starts(name, a=15):
        return A(name, a, None, 16) if name not in PART else A(name, a, PART[name][2], 16)

    lims(0)
    usum(0)
    for t in range(TV):
        p = t % 2
        AB, yv = A("AB%d" % p), A("AB%d" % p, NPOS, NPOS + Q)
        nxt = t + 1
        last = nxt == TV
        pv = ("aV%d" if t else "oV%d") % t
        Lp, V = A(pv, 0, Q), A(pv, Q, 2 * Q)
        seq = gather_l(t)
        wseq = wcount(t) if t else [scan(TH, A("MSK"), A("DL0"), 0.0, op.mult, op.add)]
        seq += gather_c(t)
        seq.append(uint())
        wseq[0]["soft"].append(seq[0])
        chain(seq)
        gather_s(t)
        tt(TA, V, TH, op.is_ge)
        tt(A("y_"), TA, V, op.add)
        ts(A("tS"), V, 15 << 18, op.bitwise_and, 9, op.arith_shift_right)
        tt(A("KEYC"), A("y_"), K21, op.add)
        tt(A("SLT"), A("tS"), KC, op.add)
        tt(A("mkL"), A("XL", 0, Q), Lp, op.min)
        scan(A("RS"), A("RSTL"), A("XS", 0, Q), -2.0 ** 20, op.min, op.max)
        scan(A("RL"), A("RSTL"), A("mkL"), -2.0 ** 20, op.min, op.max)
        RL, RC = starts("RL"), starts("RC")
        act(LF(0), LF(36), af.Copy, scale=37.0, bias=float(t))
        act(LF(1), RL, af.Copy, bias=97.0 * t)
        act(LF(10), RL, af.Copy, scale=2.0, bias=-8192.0)
        cp(LI(0, 2), A("RLS", 15, 384, 16))
        ts(LI(3), LI(0), 4095, op.bitwise_and)
        tt(LI(4, 2), LI(2, 2), LF(36, 2), op.mult)
        ts(LI(6, 2), LI(4, 2), 5, op.arith_shift_right)
        tt(LI(8, 2), LI(6, 2), LF(0, 2), op.add)
        ts(LI(10), LI(8), 4095, op.bitwise_and)
        ts(LI(11), LI(9), 3840, op.bitwise_and)
        ts(LI(12), LI(1), 15, op.bitwise_and)
        ts(LF(2), LI(12), 8192, op.mult, 4096, op.add)
        tt(LF(3), LF(2), LI(10), op.add)
        tt(LF(4), A("cv"), LI(3), op.subtract)
        tt(LF(5), LI(11), LF(4), op.add)
        tt(LF(6), LF(5), RL, op.add)
        ts(LF(7), RL, 0, op.is_lt)
        ts(LF(8), RL, 0, op.is_ge)
        tt(LF(9), LF(7), LF(3), op.mult)
        tt(LF(11), LF(6), LF(9), op.max)
        ts(LI(13), LI(0), 9, op.arith_shift_right, 240, op.bitwise_and)
        tt(LF(12), A("cp"), LI(13), op.subtract)
        ts(LF(13), LI(11), -DUMP, op.add)
        tt(TA, A("XC", 0, Q), A("KEYC"), op.min)
        tt(A("mk"), TA, A("SLT"), op.max)
        scan(A("RC"), A("RSTC"), A("mk"), -2.0 ** 27, op.min, op.max)
        if not last:
            lims(nxt)
        cp(LI(16), RC)
        ts(LF(14), RC, -2.0 ** 24, op.is_lt)
        ts(LF(15), RC, -2.0 ** 24, op.is_ge)
        ts(LI(17), LI(16), 1, op.bitwise_and)
        ts(LI(18), LI(16), 0x3FFFE, op.bitwise_and, 1, op.arith_shift_right)
        tt(LF(16), LF(14), LF(11), op.mult)
        tt(LF(17), LI(17), LI(18), op.mult)
        tt(starts("bL", 0), LF(16), LF(17), op.add)
        scan(TA, A("MSK"), A("bL"), 0.0, op.mult, op.add)
        tt(A("dif"), TA, Lp, op.subtract)
        ts(TB, A("dif"), -4096, op.max, 4096, op.min)
        tt(A("sL"), TB, Lp, op.add)
        ts(A("sM"), A("sL"), 4095, op.bitwise_and)
        if not last:
            cp(A("oL%d" % (nxt % 2)), A("sM"))
            send("L", nxt)
        tt(LF(18), LF(14), LF(8), op.mult)
        tt(LF(20), LF(12), LF(18), op.mult)
        tt(LF(21), LF(13), LF(18), op.mult)
        tt(LF(22, 2), LF(20, 2), A("cb"), op.add)
        cp(A("LST"), LF(22, 2))
        PL, NL = A("LST", 0, 12), A("LST", 12, 24)
        act(A("AB%d" % (1 - p), NPOS, NPOS + Q), AB, af.Copy, off=PL)
        act(A("nD"), A("D"), af.Relu, scale=-1.0, off=PL)
        act(A("md"), A("nD"), af.Copy, scale=-1.0)
        tt(LF(24), LF(15), LF(8), op.max)
        tt(starts("bR", 0), LF(24), RC, op.mult)
        ts(LI(19), LI(16), 0x1FDFFE, op.bitwise_and)
        ts(LI(20), LI(16), 0x3C000, op.bitwise_and)
        ts(LF(25), LI(19), 1 << 18, op.add)
        ts(LF(26), LI(20), (1 << 21) + (1 << 13), op.add)
        tt(LF(27), LF(26), LI(17), op.mult)
        tt(LF(28), LF(25), LF(27), op.max)
        tt(LF(29), LF(10), LF(14), op.mult)
        tt(LF(30), LF(28), LF(15), op.mult)
        tt(starts("bN", 0), LF(29), LF(30), op.add)
        scan(TA, A("MSK"), A("bR"), 0.0, op.mult, op.add)
        tt(A("hot"), A("mk"), TA, op.is_equal)
        scan(TB, A("MSK"), A("bN"), 0.0, op.mult, op.add)
        tt(A("dif"), TB, V, op.subtract)
        tt(TA, A("hot"), A("dif"), op.mult)
        on = "oV%d" % (nxt % 2)
        tt(A(on, Q, 2 * Q), TA, V, op.add)

        pnew(NL, yv)["bonus"] = BONUS if last else 0.0
        if last:
            break
        coff(nxt)
        send("C", nxt)
        tt(A(on, 0, Q), A("sM"), K13, op.add)
        send("V", nxt)
        yexp(1 - p)
        cp(A("Bf"), LF(15))
        mms(A("w"), [(A("GW"), A("Bf"))])
        usum(1 - p)

    dma("y", T.zp[:, :], T.P[:, 0:W], [A("P", 0, W)], [], 6.0)
    pe = TV % 2
    dma("y", T.zy[:, :], T["AB%d" % pe][:, NPOS:NPOS + Q], [A("AB%d" % pe, NPOS, NPOS + Q)], [], 2.0)
    VN = A("oV%d" % pe, Q, 2 * Q)
    cp(A("X0", 0, Q), A("sM"))
    turn(A("X0", 0, Q), "ML", "TL", "S", A("SWP", 0, Q))
    act(A("E0", 0, Q), A("SWP", 0, Q), af.Copy)
    dma("y", T.zl[:, :], T.E0[:, 0:Q], [A("E0", 0, Q)], [], 2.0)
    ts(A("tF"), VN, 1, op.arith_shift_right, 8191, op.bitwise_and)
    ts(A("tA"), A("tF"), 4096, op.is_lt)
    ts(TB, A("tF"), 1, op.add)
    tt(A("tC"), A("tA"), TB, op.mult)
    ts(A("X0", Q, 2 * Q), A("tC"), -1, op.add)
    turn(A("X0", Q, 2 * Q), "MV", "TV", "S", A("OB", 0, Q))
    ts(A("sL"), VN, 14, op.arith_shift_right, 15, op.bitwise_and)
    ts(A("X1", 0, Q), A("sL"), -1, op.mult, 15, op.add)
    ts(A("sC"), VN, 18, op.arith_shift_right, 7, op.bitwise_and)
    ts(TB, A("tF"), -4096, op.add, 0, op.max)
    tt(A("X1", Q, 2 * Q), A("sC"), TB, op.add)
    act(A("E0", Q, 2 * Q), A("OB", 0, Q), af.Copy)
    dma("y", T.zc[:, :], T.E0[:, Q:2 * Q], [A("E0", Q, 2 * Q)], [], 2.0)
    turn(A("X1"), "MO", "TO", "B", A("SWP", 0, 384))
    act(A("oB"), A("SWP", 0, 384), af.Copy)
    dma("y", T.zo[:, :], T.oB[:, 0:Q], [A("oB", 0, Q)], [], 2.0)
    dma("y", T.zb[:, :], T.oB[:, Q:2 * Q], [A("oB", Q, 2 * Q)], [], 2.0)

    succ = [[] for _ in ops]
    for o in ops:
        o["need"] = list({x["i"]: x for x in o["need"]}.values())
        o["all"] = list({x["i"]: x for x in o["need"] + o["soft"]}.values())
        for x in o["all"]:
            succ[x["i"]].append(o)
    for o in reversed(ops):
        o["pri"] = o["bonus"] + o["cost"] + o["lat"] + max([0.0] + [s["pri"] + WK for s in succ[o["i"]]])
    left = {o["i"]: len(o["all"]) for o in ops}
    free = {e: 0.0 for e in list(queues) + ["net"]}
    ready = {e: [] for e in free}
    for o in ops:
        if not left[o["i"]]:
            ready[o["e"]].append((0.0, o))
    done = []
    while len(done) < len(ops):
        best = None
        for e in ready:
            for (r, o) in ready[e]:
                k = (max(r, free[e] if e != "net" else 0.0), -o["pri"], o["i"])
                if best is None or k < best[0]:
                    best = (k, e, r, o)
        k, e, r, o = best
        ready[e].remove((r, o))
        o["st"] = k[0]
        o["fin"] = k[0] + o["cost"] + o["lat"]
        free[e] = k[0] + o["cost"]
        done.append(o)
        for s in succ[o["i"]]:
            left[s["i"]] -= 1
            if not left[s["i"]]:
                ready[s["e"]].append((max([x["fin"] + WK for x in s["need"]] + [x["fin"] for x in s["soft"]]), s))
    count = {}
    clock = {e: {} for e in queues}
    for o in done:
        e = o["e"]
        if e == "net":
            o["c"] = {}
            continue
        want = {}
        for x in o["need"]:
            if x["v"] > want.get(x["sem"], (0, None))[0]:
                want[x["sem"]] = (x["v"], x)
        ck = clock[e]
        for s in sorted(want, key=lambda s: -len(want[s][1]["c"])):
            v, x = want[s]
            if ck.get(s, 0) >= v:
                continue
            queues[e].wait_ge(T.sem[s], v)
            for k, y in x["c"].items():
                ck[k] = max(ck.get(k, 0), y)
            ck[s] = v
        ins = o["fn"](queues[e])
        if o["inc"] > 0:
            ins.then_inc(T.sem[o["sem"]], o["inc"])
        count[o["sem"]] = count.get(o["sem"], 0) + abs(o["inc"])
        o["v"] = count[o["sem"]]
        o["c"] = dict(ck)
    for s in sorted(count):
        if clock["g"].get(s, 0) < count[s]:
            g.wait_ge(T.sem[s], count[s])
